import numpy as np, ml_dtypes
CORES = [9,25,41,57]
N = 4
BF = ml_dtypes.bfloat16
def gentries(a):
    return np.ascontiguousarray(a.reshape(8, 16, -1).transpose(0, 2, 1)).reshape(8, -1)
def gtable(e):
    e = np.asarray(e); return np.ascontiguousarray(e.reshape(8, -1, 16).transpose(0, 2, 1)).reshape(128, -1).astype(np.int32)
L, A, B, H, RO, K = 2048, 256, 3, 1, 2, 11
def woven(rng, lens, ring):
    lens = np.asarray(lens); e = np.add.accumulate(lens); s = e - lens; ring = np.asarray(ring) & (lens > 2)
    nx = np.arange(1, L + 1); nx[e - 1] = np.where(ring, s, L)
    pv = np.arange(-1, L - 1); pv[s] = np.where(ring, e - 1, L)
    p = np.append(rng.permutation(L), L); a = np.zeros((2, L), np.int64); a[0, p[:L]] = p[nx]; a[1, p[:L]] = p[pv]
    return np.where(rng.random(L) < 0.5, a[::-1], a), p[:L]
def hills(rng, lens, p):
    lens = np.asarray(lens); k = np.repeat(np.arange(len(lens)), lens); at = np.arange(L) - (np.add.accumulate(lens) - lens)[k]; sh = (len(lens), 16)
    top = rng.random(sh) * lens[:, None]; steep = np.minimum(np.exp2(1 + 5 * rng.random(sh)) * np.power(lens.astype(np.float64), -1.0)[:, None], 0.5); high = 0.3 + 0.7 * rng.random(sh)
    v = high[k] * np.maximum(np.exp(-np.abs(at[:, None] - top[k]) * steep[k]), 0.05) * (0.5 + 0.5 * rng.random((L, 16)))
    x = np.zeros((L, 16), np.int32); x[p] = np.floor(255 * v).astype(np.int32)
    return x
def cands(rng, a):
    free = (a[0] == L) | (a[1] == L); own = np.arange(L); c = np.zeros((B + H, L), np.int64)
    for i in range(B):
        o = np.argsort(rng.random(L) + np.where(free, 0.0, 1.0) * (rng.random(L) < 0.8)); c[i, o[0::2]] = o[1::2]; c[i, o[1::2]] = o[0::2]
        u = rng.random(L); w = a[rng.integers(0, 2, L), own]
        c[i] = np.where(u < 0.15, rng.integers(0, L, L), np.where((u < 0.3) & (w < L), w, np.where((u > 0.3) & (u < 0.32), own, c[i])))
    c[B:] = rng.integers(0, A, (H, L))
    return c
def cuts(rng, n, span):
    o = np.sort(rng.permutation(span - 1)[:n - 1]) + 1
    return np.diff(np.concatenate([[0], o, [L]]))
def ends(rng, n):
    if n < 2: return np.array([1] * n + [L - n]), np.array([False] * n + [True])
    one = n % 2; h = n // 2; rest = L - one - 2 * h; o = np.sort(rng.integers(0, rest + 1, h - 1))
    lens = np.concatenate([np.ones(one, np.int64), 2 + np.diff(np.concatenate([[0], o, [rest]]))])
    return lens, np.zeros(len(lens), bool)
def common(rng, q):
    n = (3, 12, 60, 150)[(q + q // 8) % 4]
    return cuts(rng, n, int(L * (0.3 + 0.6 * rng.random()))), rng.random(n) < 0.2
def parts(rng, form, bind=None):
    M, X, C = [], [], []
    for q in range(8 * N):
        lens, ring = form(rng, q); a, p = woven(rng, lens, ring); x = hills(rng, lens, p); c = cands(rng, a)
        if bind is not None: bind(q, lens, p, x, c)
        M.append(a); X.append(x); C.append(c)
    return np.stack(M), np.stack(X), np.stack(C)
def levels(rng, M, X, C, share, hold=False, bump=0, still=None, fix=None):
    th, left = [], []; still = np.zeros(8 * N, bool) if still is None else still; fix = np.full((8 * N, RO), -1) if fix is None else fix
    for t in range(RO):
        m, E, W = walks(M, X); v = np.sort(np.where(m < L, W, 0), axis=1); c = np.add.reduce((m < L).astype(np.int64), axis=1)
        i = np.clip(2 * L - 1 - np.floor(share * c).astype(np.int64), 0, 2 * L - 1)
        b = np.clip(v[np.arange(8 * N), i] + rng.integers(0, bump + 1, 8 * N), 1, 8160)
        if hold and t == 0: b = np.full(8 * N, 8192)
        b = np.where(still, 8192, b); b = np.where(fix[:, t] >= 0, fix[:, t], b); th.append(b)
        m = np.where((m < L) & (W >= b[:, None]), L, m); left.append(np.add.reduce(((m[:, :L] == L) | (m[:, L:] == L)).astype(np.int64), axis=1))
        if t < RO - 1: M, X = turn(C, X, E, m)
    assert np.all(left[-1][still] <= np.minimum(A, left[0][still]) * 3 // 4)
    return np.stack(th, axis=1)
def pack(M, X, C, th):
    return {"nb": np.stack([gtable(a) for a in M.reshape(N, 8, -1)]), "cd": np.stack([gtable(a) for a in C.reshape(N, 8, -1)]),
            "th": np.repeat(th, 16, axis=0).reshape(N, 128, RO).astype(np.int32), "x0": np.ascontiguousarray(X.transpose(0, 2, 1)).reshape(N, 128, L).astype(np.float32).astype(BF)}
def setup_inputs(rng):
    M, X, C = parts(rng, common)
    return pack(M, X, C, levels(rng, M, X, C, 0.02 + 0.28 * rng.random(8 * N)))
def setup_inputs_room(rng):
    q = np.arange(8 * N); still = (q % 8 == 1) | (q % 8 == 4) | (q % 8 == 6); fall = (q % 8 == 7) & (q // 8 % (H + 1) < H)
    size = np.where(still, np.array([A, A + 1, A // 2])[(q // 8 + q % 8) % 3], np.array([A, A + 1, A - 1, 0, 1, 2 * A, A, A + 1])[(q + q // 8) % 8])
    size = np.where(q % 8 == 7, np.where(fall, A - 16, 2 * A), size); fix = np.where((q % 8 == 7)[:, None], rng.integers(8161, 8193, (8 * N, RO)), -1)
    def bind(q, lens, p, x, c):
        e = np.add.accumulate(lens); s = e - lens
        if q % 8 == 7:
            u, w = p[e - 1], p[s]; x[w] = 255
            if fall[q]:
                f = np.roll(w, -1); x[u] = 255; c[:B, u] = f; c[:B, f] = u
                if q // 8 >= N // 2: c[:B, u[:4]] = u[:4]; c[:B, f[:4]] = f[:4]
            else:
                c[:B, u] = u; c[:B, w] = p[s + 1]; c[B:, u] = rng.integers(0, A - 16, (H, len(u))); c[B:, u[0]] = A - 17; c[B:, w] = rng.integers(A - 16, A, (H, len(w)))
            return
        if not still[q]: return
        k = np.nonzero(lens > 1)[0]; k = k[:len(k) // 2 * 2]
        i, j = k[0::2], k[1::2]; u, v, w = p[e[i] - 1], p[e[j] - 1], p[s[i]]
        big = np.maximum.reduceat(x[p], s, axis=0); x[u] = np.maximum(big[i], big[j]); x[v] = x[u]
        c[:B, u] = v; c[:B, v] = u; c[:B, w] = w
        for d in range(1, H + 1):
            top = min(A, int(size[(q - 8 * d) % (8 * N)])); c[B + d - 1, w] = rng.integers(top * 3 // 4, top, len(w)); c[B + d - 1, w[0]] = top - 1
    M, X, C = parts(rng, lambda rng, q: ends(rng, int(size[q])), bind)
    return pack(M, X, C, levels(rng, M, X, C, 0.02 + 0.28 * rng.random(8 * N), hold=True, still=still, fix=fix))
def setup_inputs_ties(rng):
    M, X, C = parts(rng, common); X = X // 64 * 85
    return pack(M, X, C, levels(rng, M, X, C, 0.02 + 0.28 * rng.random(8 * N), bump=1))
def setup_inputs_rings(rng):
    def form(rng, q):
        i = (q + q // 8) % 8; k = L // 3
        if i == 0: lens = [L]
        elif i == 1: lens = [1, L - 1]
        elif i == 2: lens = [L]
        elif i == 3: lens = [3] * k + [L - 3 * k] * int(L > 3 * k)
        elif i == 4: lens = [2] * (L // 2)
        elif i == 5: lens = cuts(rng, 40, L // 2)
        elif i == 6: lens = [1] * L
        else: lens = cuts(rng, 60, L // 2)
        return np.array(lens), (rng.random(len(lens)) < 0.5) if i == 7 else np.full(len(lens), i != 2)
    M, X, C = parts(rng, form); X = rng.integers(0, 16, (8 * N, L, 16)).astype(np.int32)
    X[np.arange(8 * N)[:, None], rng.integers(0, L, (8 * N, 16)), np.arange(16)] = rng.integers(100, 256, (8 * N, 16))
    fix = np.full((8 * N, RO), -1)
    for q in range(8 * N):
        i = (q + q // 8) % 8
        if q // 8 % 2 == 0 and i == 4:
            X[q] = np.where(np.arange(L) < np.minimum(M[q, 0], M[q, 1]), 255, 0)[:, None]; fix[q] = (8161, 8192)[q // 16 % 2]
        if q // 8 % 2 == 0 and i == 6:
            o = rng.permutation(L); u, v = o[0::2], o[1::2]; c = C[q]; c[:B, u] = v; c[:B, v] = v; c[B - 1, v] = u
            x = rng.integers(64, 256, (L, 16)); x[v] = x[u]; X[q] = x; fix[q] = 8192
    return pack(M, X, C, levels(rng, M, X, C, 0.02 + 0.28 * rng.random(8 * N), bump=1, fix=fix))
def setup_inputs_alike(rng):
    M, X, C = parts(rng, common); own = np.arange(L); fix = np.full((8 * N, RO), -1)
    for q in range(8 * N):
        g = q % 8
        if g < 2: C[q, :B] = rng.choice(np.array([0, L - 1, L // 2, 3]), (B, L))
        if g == 2: w = M[q][rng.integers(0, 2, (B, L)), own]; C[q, :B] = np.where(w < L, w, own)
        if g in (3, 4): C[q, 1:B] = C[q, 0]
        if g == 5: X[q] = 77
        if g == 5 and q // 8 % 2 == 0: fix[q, 0] = 0
        if g % 2 == 0: C[q, B:] = rng.choice(np.array([0, 1, A - 1]), (H, L))
    return pack(M, X, C, levels(rng, M, X, C, 0.02 + 0.28 * rng.random(8 * N), fix=fix))
def setup_inputs_spread(rng):
    M, X, C = parts(rng, common)
    v = 256 * rng.random((8 * N, L, 16)) * np.exp2(-rng.integers(0, 9, (8 * N, L, 1))) * (rng.random((8 * N, L, 1)) > 0.0625)
    X = np.minimum(np.floor(v), 255).astype(np.int32)
    return pack(M, X, C, levels(rng, M, X, C, rng.random(8 * N) ** 3))
def check_inputs(d):
    bad = []; G = np.arange(8 * N)[:, None]; own = np.arange(L)
    M = np.stack([gentries(a) for a in d["nb"]]).astype(np.int64).reshape(8 * N, 2, L); C = np.stack([gentries(a) for a in d["cd"]]).astype(np.int64).reshape(8 * N, B + H, L)
    if np.min(M) < 0 or np.max(M) > L: bad.append("range of nb")
    else:
        if np.any(M == own): bad.append("nb: a layer linked to itself")
        if np.any((M[:, 0] == M[:, 1]) & (M[:, 0] < L)): bad.append("nb: both slots name one layer")
        P = np.concatenate([M, np.full((8 * N, 2, 1), L)], axis=2)
        for s in range(2):
            m = M[:, s]
            if not np.all((m == L) | (P[:, 0][G, m] == own) | (P[:, 1][G, m] == own)): bad.append("nb: a link of one side only, slot " + str(s))
    if np.min(C) < 0 or np.max(C[:, :B]) > L - 1 or np.max(C[:, B:]) > A - 1: bad.append("range of cd")
    t = d["th"].reshape(8 * N, 16, RO)
    if np.min(t) < 0 or np.max(t) > 8192: bad.append("range of th")
    if np.any(t != t[:, :1]): bad.append("th: rows of a group that differ")
    v = d["x0"].astype(np.float32)
    if not np.all((v >= 0) & (v <= 255) & (v == np.floor(v))): bad.append("x0: whole numbers from 0 to 255")
    return bad
def walks(M, X):
    Q = len(M); G = np.arange(Q)[:, None]; m = M.reshape(Q, 2 * L)
    came = np.concatenate([M[:, 0], np.full((Q, 1), L)], axis=1)[G, m] == np.tile(np.arange(L), 2)
    back = np.where(m < L, np.where(came, m, L + m), 2 * L)
    step = np.concatenate([np.where(m < L, np.where(came, L + m, m), 2 * L), np.full((Q, 1), 2 * L)], axis=1)
    E = np.concatenate([X, X, np.zeros((Q, 1, 16), X.dtype)], axis=1); P = step[G, step]
    for k in range(K):
        E = np.maximum(E, E[G, P]); P = P[G, P]
    D = np.add.reduce(np.abs(E - E[G, step]), axis=2)
    return m, E, D[:, :2 * L] + D[G, back]
def turn(C, X, E, m):
    Q = len(X); G = np.arange(Q)[:, None]; own = np.arange(L); M = m.reshape(Q, 2, L)
    X = (X + np.abs(E[:, :L] - E[:, L:2 * L])) >> 1
    free = (M[:, 0] == L) | (M[:, 1] == L); place = np.add.accumulate(free.astype(np.int64), axis=1) - 1
    q, n = np.nonzero(free & (place < A)); S = np.zeros((Q, A, 16), X.dtype); S[q, place[q, n]] = X[q, n]
    S = S.reshape(N, 8, A, 16)
    come = [np.roll(S, d, axis=0).reshape(Q, A, 16)[G, C[:, B + d - 1]] for d in range(1, H + 1)]
    far = []
    for i in range(B):
        c = C[:, i]; ok = free[G, c] & (c != own) & (c != M[:, 0]) & (c != M[:, 1])
        far.append(np.where(ok, np.add.reduce(np.abs(X - X[G, c]), axis=2), 2 ** 20))
    for v in come: far.append(np.add.reduce(np.abs(X - v), axis=2))
    pick = np.argmin(np.stack(far, axis=1), axis=1)
    to = np.where(free & (pick < B), np.take_along_axis(C, pick[:, None, :], 1)[:, 0], L)
    both = (to < L) & (np.concatenate([to, np.full((Q, 1), L)], axis=1)[G, to] == own); low = M[:, 0] == L
    M = np.stack([np.where(both & low, to, M[:, 0]), np.where(both & ~low, to, M[:, 1])], axis=1)
    for d, v in enumerate(come): X = np.where((free & (pick == B + d))[:, :, None], (X + v) >> 1, X)
    return M, X
def reference(nb, cd, th, x0):
    M = np.stack([gentries(a) for a in nb]).astype(np.int64).reshape(8 * N, 2, L); C = np.stack([gentries(a) for a in cd]).astype(np.int64).reshape(8 * N, B + H, L)
    X = np.ascontiguousarray(x0.astype(np.float32).reshape(8 * N, 16, L).transpose(0, 2, 1)).astype(np.int32); t = th.astype(np.int64).reshape(8 * N, 16, RO)[:, 0]
    for rnd in range(RO):
        m, E, W = walks(M, X)
        M, X = turn(C, X, E, np.where((m < L) & (W >= t[:, rnd:rnd + 1]), L, m))
    return {"yn": np.stack([gtable(a) for a in M.reshape(N, 8, 2 * L)]).astype(np.float32), "yx": np.ascontiguousarray(X.transpose(0, 2, 1)).reshape(N, 128, L).astype(np.float32).astype(BF)}

@@ -1,0 +1,615 @@
+from concourse.mybir import AluOpType as Op, AxisListType as AX, ActivationFunctionType as AF
+
+L = 2048
+A = 256
+RO = 2
+K = 10
+FREE = 2063
+END = FREE + L
+OFF = 16.25
+C16A, C16B = 2.0 ** 27 - 8, 2.0 ** 27 + 16
+M64 = 805306368.0
+M1 = 12582912.0
+HALF = 0.5 - 2.0 ** -11
+BF, F, I, U = "bfloat16", "float32", "int32", "uint16"
+WN = ["TWO", "PTR", "SUM", "SUMH", "SUMK", "SUMN", "SWW", "R0", "R1"]
+IDS = [256.0, 0.0625, 3968.0, 128.0, -128.0, 1.0, 2048.0, -2048.0, -1.0, 8192.0, -8192.0, 16384.0, -16384.0, 16.0, 0.5,
+       2.0 ** 26, -2.0 ** 28]
+CST = [3 * 2.0 ** 24, 2048.0, 4096.0, 15 * 2.0 ** 24, 6144.0]
+NV = 5
+HI, LO, CAME, LESS, OPEN, LOW, MIX, JOIN = range(8)
+
+SCRATCH = {
+    "nbi": ("sbuf", [128, 256], I), "cdi": ("sbuf", [128, 512], I), "thi": ("sbuf", [128, 2], I),
+    "thf": ("sbuf", [128, 2], F),
+    "X": ("sbuf", [128, L], BF), "EA": ("sbuf", [128, 4112], BF), "EB": ("sbuf", [128, 4112], BF),
+    "EC": ("sbuf", [128, 4096], BF),
+    "PA": ("sbuf", [128, 4112], BF), "PB": ("sbuf", [128, 4112], BF), "PS": ("sbuf", [128, 4112], BF),
+    "XW0": ("sbuf", [128, A + L + 16], BF), "XW1": ("sbuf", [128, A + L + 16], BF),
+    "blk0": ("sbuf", [128, A], BF), "blk1": ("sbuf", [128, A], BF),
+    "ab": ("sbuf", [128, L], BF), "rr": ("sbuf", [128, L], BF), "rg": ("sbuf", [128, L], BF), "y32": ("sbuf", [128, L], F),
+    "MC": ("sbuf", [128, 4 * L], BF), "SC": ("sbuf", [128, 4 * L], BF),
+    "wide": ("sbuf", [128, 144 * len(WN)], BF), "idm": ("sbuf", [128, 128 * len(IDS)], BF),
+    "blkm": ("sbuf", [128, 128], BF), "utm": ("sbuf", [128, 128], BF), "zer": ("sbuf", [128, 128], BF),
+    "blkf": ("sbuf", [128, 128], BF), "oneb": ("sbuf", [128, 128], BF),
+    "cst": ("sbuf", [128, 128 * len(CST)], BF), "mh": ("sbuf", [128, 512], BF),
+    "pi": ("sbuf", [128, 4], I), "col": ("sbuf", [128, 32], F), "b9": ("sbuf", [128, 16], F),
+    "rk": ("sbuf", [128, 256], F), "r16": ("sbuf", [128, 256], BF),
+    "nio": ("sbuf", [128, 256], F), "kcol": ("sbuf", [128, 16], F),
+    "m": ("sbuf", [128, 256], F), "c": ("sbuf", [128, 256], BF), "fr": ("sbuf", [128, 256], BF),
+    "hb": ("sbuf", [128, 256], BF), "lb": ("sbuf", [128, 256], BF), "l0": ("sbuf", [128, 256], BF),
+    "hs": ("sbuf", [128, 128], BF), "ls": ("sbuf", [128, 128], BF),
+    "hw": ("sbuf", [128, 128], BF), "lw": ("sbuf", [128, 128], BF),
+    "t1": ("sbuf", [128, 256], F), "t2": ("sbuf", [128, 256], F), "nn": ("sbuf", [128, 256], F),
+    "bf": ("sbuf", [128, 256], F), "s01": ("sbuf", [128, 128], F),
+    "wl": ("sbuf", [128, 256], U), "sl": ("sbuf", [128, 256], U), "bl": ("sbuf", [128, 256], U),
+    "pl0": ("sbuf", [128, 256], U), "pl1": ("sbuf", [128, 256], U),
+    "cl": ("sbuf", [128, 512], U), "wcl": ("sbuf", [128, 384], U), "cf": ("sbuf", [128, 384], F),
+    "hc": ("sbuf", [128, 384], BF), "lc": ("sbuf", [128, 384], BF), "lz": ("sbuf", [128, 384], BF),
+    "es": ("sbuf", [128, 384], BF), "eq": ("sbuf", [128, 768], BF), "ep": ("sbuf", [128, 768], BF),
+    "sw": ("sbuf", [128, 128 * NV], F),
+    "d1": ("sbuf", [128, 128], F), "d2": ("sbuf", [128, 128], F), "ml32": ("sbuf", [128, 128], F),
+    "fb": ("sbuf", [128, 128], BF), "cum": ("sbuf", [128, 128], F), "pw": ("sbuf", [128, 144], F),
+    "one": ("sbuf", [128, 128], F), "sg": ("sbuf", [128, 2048], BF), "acc": ("sbuf", [128, 16], F),
+    "colb": ("sbuf", [128, 16], BF), "l1": ("sbuf", [128, 16], U), "l2": ("sbuf", [128, 16], U),
+    "cmp": ("sbuf", [128, 256], BF),
+    "km": ("sbuf", [128, 128], F), "ki": ("sbuf", [128, 128], I), "ti": ("sbuf", [128, 128], I),
+    "tq": ("sbuf", [128, 128], F), "to": ("sbuf", [128, 128], F), "tl": ("sbuf", [128, 128], U),
+    "ml": ("sbuf", [128, 128], U), "mix": ("sbuf", [128, 128], BF),
+    "wa": ("sbuf", [128, 256], F), "jb": ("sbuf", [128, 256], BF), "jj": ("sbuf", [128, 256], F),
+    "e0": ("sbuf", [128, 256], BF), "yo": ("sbuf", [128, 256], F),
+}
+for _b in range(8):
+    SCRATCH["q%d" % _b] = ("psum", [128, 512], F)
+NDMA = 48
+SEMAPHORES = (["sv", "sa", "sp", "sg", "sent"] + ["arr%d" % t for t in range(RO)] + ["ec%d" % i for i in range(4)]
+              + ["dm%d" % i for i in range(NDMA)])
+
+
+def rank_program(g, core, T, topo):
+    rank = T.rank_of(core)
+    if rank is None:
+        return
+    nxt = T.cores[(rank + 1) % len(T.cores)]
+    Q = {"v": g.vector, "a": g.scalar, "p": g.tensor, "s": g.sync, "g": g}
+    cnt = {"sv": 0, "sa": 0, "sp": 0, "sg": 0}
+    known = {e: {} for e in Q}
+    clock = {}
+    hist = {}
+    ndma = [0]
+
+    def R(name, a=0, b=None, step=1, row=None):
+        t = T[name]
+        if b is None:
+            b = t.shape[1]
+        cs = slice(a, b) if step == 1 else slice(a, b, step)
+        return (t[:, cs] if row is None else t[row::16, cs], name, a, b, row)
+
+    def B(name, i, n=128):
+        return R(name, n * i, n * i + n)
+
+    def wait(e, tok):
+        s, n = tok
+        if known[e].get(s, 0) >= n:
+            return
+        Q[e].wait_ge(T.sem[s], n)
+        known[e][s] = n
+        for s2, n2 in clock.get(tok, {}).items():
+            if known[e].get(s2, 0) < n2:
+                known[e][s2] = n2
+
+    def order(e, reads, writes, cont=False):
+        need = {}
+        for lst, w in ((reads, False), (writes, True)):
+            for r in lst:
+                ps = r[1][0] == "q"
+                for a, b, row, w2, tok, e2 in hist.get(r[1], []):
+                    if ps:
+                        if e2 == e and ((e == "p" and cont) or not (w or w2)):
+                            continue
+                    elif not (w or w2) or b <= r[2] or r[3] <= a or (row is not None and r[4] is not None and row != r[4]):
+                        continue
+                    need[tok[0]] = max(need.get(tok[0], 0), tok[1])
+        for s, n in need.items():
+            wait(e, (s, n))
+
+    def note(e, tok, reads, writes):
+        clock[tok] = dict(known[e])
+        for lst, w in ((reads, False), (writes, True)):
+            for r in lst:
+                h = hist.setdefault(r[1], [])
+                if w:
+                    h[:] = [x for x in h if not (r[1][0] == "q" or (r[2] <= x[0] and x[1] <= r[3] and (r[4] is None or r[4] == x[2])))]
+                h.append((r[2], r[3], r[4], w, tok, e))
+
+    def run(e, reads, writes, call, cont=False):
+        reads = [r for r in reads if isinstance(r, tuple)]
+        order(e, reads, writes, cont)
+        s = "s" + e
+        cnt[s] += 1
+        call().then_inc(T.sem[s], 1)
+        note(e, (s, cnt[s]), reads, writes)
+
+    def ap(x):
+        return x[0] if isinstance(x, tuple) else x
+
+    def dma(out, in_, e="s", s=None):
+        reads = [in_] if isinstance(in_, tuple) else []
+        writes = [out] if isinstance(out, tuple) else []
+        order(e, reads, writes)
+        if s is None:
+            s = "dm%d" % ndma[0]
+            ndma[0] += 1
+        elif cnt.get(s):
+            wait(e, (s, cnt[s]))
+        Q[e].dma_start(ap(out), ap(in_)).then_inc(T.sem[s], 16)
+        cnt[s] = cnt.get(s, 0) + 16
+        note(e, (s, cnt[s]), reads, writes)
+
+    def unwrap(row, src, a=0):
+        dma(R("PS", a, a + 16 * (src[3] - src[2]), row=row), src)
+
+    def ts(out, in0, s1, op0, s2=None, op1=None):
+        if op1 is None:
+            run("v", [in0, s1], [out], lambda: g.vector.tensor_scalar(out[0], in0[0], ap(s1), None, op0))
+        else:
+            run("v", [in0, s1, s2], [out], lambda: g.vector.tensor_scalar(out[0], in0[0], ap(s1), ap(s2), op0, op1))
+
+    def tt(out, in0, in1, op):
+        run("v", [in0, in1], [out], lambda: g.vector.tensor_tensor(out[0], in0[0], in1[0], op))
+
+    def cp(out, in_):
+        run("v", [in_], [out], lambda: g.vector.tensor_copy(out[0], in_[0]))
+
+    def total(out, in_):
+        run("v", [in_], [out], lambda: g.vector.tensor_reduce(out[0], in_[0], AX.X, Op.add))
+
+    def fill(out, val):
+        run("v", [], [out], lambda: g.vector.memset(out[0], val))
+
+    def act(out, in_, func=AF.Identity, bias=0.0, scale=1.0, accum=None):
+        w = [out] + ([accum] if accum else [])
+        if accum:
+            run("a", [in_, bias, scale], w, lambda: g.scalar.activation(out[0], in_[0], func, ap(bias), ap(scale), accum_out=accum[0]))
+        else:
+            run("a", [in_, bias, scale], w, lambda: g.scalar.activation(out[0], in_[0], func, ap(bias), ap(scale)))
+
+    def gat(e, out, win, off, in1=None, op=None):
+        if e == "a":
+            run("a", [win, off], [out], lambda: g.scalar.activation(out[0], win[0].indirect(off[0]), AF.Copy))
+        elif in1 is None:
+            run("v", [win, off], [out], lambda: g.vector.tensor_copy(out[0], win[0].indirect(off[0])))
+        else:
+            run("v", [win, off, in1], [out], lambda: g.vector.tensor_tensor(out[0], win[0].indirect(off[0]), in1[0], op))
+
+    def mm(out, terms, start=True, stop=True):
+        def call():
+            for i, (l, r) in enumerate(terms):
+                ins = g.tensor.matmul(out[0], l[0], r[0], start and i == 0, stop and i == len(terms) - 1)
+            return ins
+        run("p", [x for t in terms for x in t], [out], call, cont=not start)
+
+    def wrap(w, name, a, b):
+        o = 144 * WN.index(w)
+        return [(R("wide", o + 15 - i, o + 143 - i), R(name, a + i, b, 16)) for i in range(16)]
+
+    def iota(out, pattern, base, cm, flt=True):
+        if flt:
+            run("g", [], [out], lambda: g.iota(out[0], pattern, base, cm, allow_small_or_imprecise_dtypes=True))
+        else:
+            run("g", [], [out], lambda: g.iota(out[0], pattern, base, cm))
+
+    def select(out, in_, pattern, op, val, base, cm):
+        run("g", [in_], [out], lambda: g.affine_select(out[0], in_[0], pattern, op, val, base, cm))
+
+    def ID(val):
+        return B("idm", IDS.index(val))
+
+    def C(k):
+        return R("col", k, k + 1)
+
+    def ROW(r):
+        return C(3 + r)
+
+    def hi16(h, src):
+        ts(h, src, C16A, Op.add, C16B, Op.subtract)
+
+    def hi64(h, src):
+        ts(h, src, M64, Op.add, M64, Op.subtract)
+
+    def widen(w, scale):
+        o = 144 * WN.index(w)
+        act(R("wide", o + 15, o + 144, 16), R("b9", 0, 9), AF.Identity, 0.0, scale)
+
+    def steplist(t):
+        mm(R("q6", 0, 256), [(ID(256.0), R("lb")), (ID(0.0625), R("hb")), (ID(128.0), R("c"))] + ([(ID(-128.0), R("e0"))] if t else []))
+        ts(R("wl"), R("q6", 0, 256), -256 * OFF, Op.add)
+
+    def laterlists(t):
+        mm(R("q7", 0, 256), [(ID(256.0), R("lb")), (ID(0.0625), R("hb")), (ID(-128.0), R("c"))] + ([(ID(128.0), R("e0"))] if t else []))
+        mm(R("q6", 256, 512), [(ID(1.0), R("lb")), (ID(1.0), R("hb")), (ID(2048.0), R("c"))] + ([(ID(-2048.0), R("e0"))] if t else []))
+
+    def laterlists2():
+        ts(R("bl"), R("q7", 0, 256), 128 - 256 * OFF, Op.add)
+        ts(R("sl"), R("q6", 256, 512), -OFF, Op.add)
+
+    dma(R("nbi"), T.nb[:])
+    dma(R("cdi"), T.cd[:], "a")
+    dma(R("thi"), T.th[:], "a")
+    dma(R("X"), T.x0[:], "a")
+    iota(R("pi", 0, 1), [[0, 1]], 0, 1, False)
+    iota(R("b9"), [[1, 16]], 0, 0)
+    iota(R("zer"), [[0, 128]], 0, 0)
+    for val in IDS[:3]:
+        select(ID(val), R("zer"), [[-1, 128]], Op.not_equal, val, 0, 1)
+    iota(R("r16"), [[0, 2], [16, 128]], 0, 0)
+    for val in IDS[3:]:
+        select(ID(val), R("zer"), [[-1, 128]], Op.not_equal, val, 0, 1)
+    for w in ("EA", "EB", "PA", "PB"):
+        iota(R(w, 4096, 4112), [[0, 16]], 0, 0)
+    iota(R("rk"), [[1, 256]], 0, 0)
+    iota(R("one"), [[0, 128]], 1, 0)
+    iota(R("oneb"), [[0, 128]], 1, 0)
+    select(R("utm"), R("oneb"), [[-16, 8], [0, 16]], Op.is_ge, 0.0, 0, 1)
+    select(R("blkm"), R("utm"), [[16, 8], [0, 16]], Op.is_ge, 0.0, 15, -1)
+    select(R("utm"), R("blkm"), [[-1, 128]], Op.is_gt, 0.0, 0, 1)
+    for i, val in enumerate(CST):
+        select(B("cst", i), R("zer"), [[0, 128]], Op.is_gt, val, 0, 0)
+    for j in range(4):
+        select(B("mh", j), R("zer"), [[0, 128]], Op.is_gt, -0.5, 0, 0)
+    iota(R("pw", 128, 144), [[0, 16]], 65536, 0)
+    for t in range(RO):
+        iota(R("XW%d" % t, A + L, A + L + 16), [[0, 16]], 0, 0)
+    fill(R("PS", 0, L), 0.0)
+    act(R("PS", L, 2 * L), R("PS", 0, L), AF.Copy)
+    ts(R("pi", 1, 2), R("pi", 0, 1), 15, Op.bitwise_and)
+    ts(R("pi", 2, 3), R("pi", 0, 1), 4, Op.arith_shift_right)
+    fill(R("PS", 2 * L, 4112), 0.0)
+    cp(R("col", 0, 3), R("pi", 0, 3))
+    fill(R("wide"), 0.0)
+    ts(R("col", 3, 11), R("b9", 0, 8), C(1), Op.is_equal)
+    ts(C(11), C(1), 1.0, Op.is_le)
+    ts(R("t1"), R("nbi"), OFF, Op.add)
+    ts(R("fr"), R("nbi"), 2048.0, Op.is_ge)
+    hi16(R("hb"), R("t1"))
+    unwrap(HI, R("hb"))
+    ts(R("b9", 0, 9), R("b9", 0, 9), C(2), Op.is_equal)
+    tt(R("l0"), R("t1"), R("hb"), Op.subtract)
+    unwrap(LO, R("l0"))
+    dma(R("EA", 0, L), T.x0[:])
+    dma(R("EA", L, 2 * L), T.x0[:])
+    mm(R("q6", 0, 256), [(ID(256.0), R("l0")), (ID(0.0625), R("hb")), (ID(3968.0), R("fr"))])
+    ts(C(12), ROW(LO), 15 + OFF, Op.mult, ROW(CAME), Op.add)
+    ts(R("t2"), R("fr"), FREE + OFF, Op.mult)
+    ts(C(13), ROW(HI), 2048.0, Op.mult, ROW(OPEN), Op.add)
+    ts(R("wl"), R("q6", 0, 256), -256 * OFF, Op.add)
+    ts(R("PS", 4096, 4097), C(12), C(13), Op.add)
+    widen("TWO", C(11))
+    ts(R("nio"), R("r16"), C(1), Op.add, OFF, Op.add)
+    tt(R("nn"), R("t2"), R("nio"), Op.max)
+    for j in (0, 2, 3, 1):
+        gat("va"[j // 2], B("PA", j, 1024), R("PS"), B("wl", j, 64))
+        mm(B("q%d" % (j // 2), j % 2, 64), wrap("TWO", "PA", 1024 * j, 1024 * j + 1024))
+    tt(R("m"), R("t1"), R("t2"), Op.max)
+    unwrap(OPEN, R("fr"))
+    tt(B("c", 1), R("q1", 0, 128), B("nn", 1), Op.is_equal)
+    tt(R("lb"), R("m"), R("hb"), Op.subtract)
+    unwrap(LO, R("lb"))
+    tt(B("c", 0), R("q0", 0, 128), B("nn", 0), Op.is_equal)
+    unwrap(CAME, R("c"))
+    ts(C(14), ROW(CAME), 2048.0, Op.mult, C(11), Op.add)
+    steplist(0)
+    ts(C(14), ROW(LESS), -2048.0, Op.mult, C(14), Op.add)
+    widen("PTR", C(14))
+    act(R("PA", END, END + 1), R("PS", 4096, 4097), AF.Copy)
+    act(R("PB", END, END + 1), R("PS", 4096, 4097), AF.Copy)
+    act(R("d2"), R("nio", 0, 128), AF.Identity, A - OFF)
+    ts(C(15), C(11), -8192.0, Op.mult)
+    ts(C(17), ROW(MIX), 4096.0, Op.mult, C(11), Op.add)
+    ts(C(20), ROW(JOIN), ROW(OPEN), Op.subtract, 512.0, Op.mult)
+    ts(C(16), ROW(CAME), -2.0 ** 26, Op.mult, C(15), Op.add)
+    ts(C(18), ROW(LOW), 0.5, Op.mult, C(17), Op.add)
+    ts(C(19), C(1), 8192 + OFF, Op.add)
+    ts(R("thf"), R("thi"), 0.5, Op.mult)
+    ts(R("cf"), R("cdi", 0, 384), OFF, Op.add)
+    cp(R("cl"), R("cdi"))
+    hi16(R("hc"), R("cf"))
+    tt(R("lc"), R("cf"), R("hc"), Op.subtract)
+
+    for t in range(RO):
+        last = t == RO - 1
+        XW = "XW%d" % t
+
+        def point(k, h):
+            src, dst = ("PA", "PB")[(k - 1) % 2], ("PA", "PB")[k % 2]
+            gat("a", B(dst, h, L), R(src), B("pl%d" % ((k - 1) % 2), h))
+            mm(R("q%d" % h, 0, 128), wrap("PTR", dst, h * L, h * L + L))
+
+        def conv(k, h):
+            ts(B("pl%d" % (k % 2), h), R("q%d" % h, 0, 128), -OFF, Op.add)
+
+        def most(k, j):
+            es, ed = ("EA", "EB")[k % 2], ("EB", "EA")[k % 2]
+            own = B("X", j % 2, 1024) if k == 0 else B("EC", j, 1024)
+            gat("v", B(ed, j, 1024), R(es), B("pl%d" % (k % 2), j, 64), own, Op.max)
+            dma(B("EC", j, 1024), B(ed, j, 1024), "s", "ec%d" % j)
+
+        def ended(j):
+            mm(R("q%d" % (2 + j % 2)), [(R("blkf"), B("PB", j, 512)), (R("blkf"), B("PB", 4 + j, 512))])
+            act(B("rg", j, 512), R("q%d" % (2 + j % 2)), AF.Copy)
+
+        def fold1(j):
+            mm(R("q%d" % (2 + j % 2)), [(ID(1.0), B("EA", j, 512)), (ID(-1.0), B("EA", 4 + j, 512))])
+            act(B("ab", j, 512), R("q%d" % (2 + j % 2)), AF.Abs)
+
+        def fold2(j):
+            mm(R("q%d" % (4 + j % 2)), [(ID(1.0), B("rg", j, 512)), (ID(1.0), B("ab", j, 512))])
+            act(B("rr", j, 512), R("q%d" % (4 + j % 2)), AF.Relu)
+
+        def fold3(j):
+            mm(R("q%d" % (7 * (j % 2))), [(ID(1.0), B("X", j, 512)), (ID(1.0), B("ab", j, 512)), (ID(-1.0), B("rr", j, 512))])
+            act(B("y32", j, 512), R("q%d" % (7 * (j % 2))), AF.Identity, M1, HALF)
+
+        def fold4(h):
+            act(R(XW, A + 1024 * h, A + 1024 * h + 1024), B("y32", h, 1024), AF.Identity, -M1)
+            dma(B("X", h, 1024), R(XW, A + 1024 * h, A + 1024 * h + 1024), "g")
+
+        def sums(h):
+            mm(B("q6", h, 64), wrap("SUMH", "EA", 1024 * h, 1024 * h + 1024) + wrap("SUMH", "EA", L + 1024 * h, L + 1024 * h + 1024), True, False)
+
+        def sums2(h):
+            mm(B("q6", h, 64), wrap("SUMH", "rr", 1024 * h, 1024 * h + 1024), False, True)
+
+        def larger(j):
+            gat("v", B("EB", j, 1024), R("EA"), B("sl", j, 64), B("EC", j, 1024), Op.max)
+
+        def largersum(j):
+            mm(B("q%d" % (j // 2), j % 2, 64), wrap("SUM", "EB", 1024 * j, 1024 * j + 1024))
+        for k in range(K):
+            if k == 0:
+                laterlists(t)
+                for j in range(4):
+                    gat("a", B("PA", j, 1024), R("PS"), B("wl", j, 64))
+                    mm(R("q%d" % (j % 2), 0, 64), wrap("PTR", "PA", 1024 * j, 1024 * j + 1024))
+                    ts(B("pl0", j, 64), R("q%d" % (j % 2), 0, 64), -OFF, Op.add)
+                    if j:
+                        most(k, j - 1)
+                    if t == 0 and j == 0:
+                        mm(R("q4", 0, 384), [(ID(128.0), R("lc")), (ID(0.0625), R("hc"))])
+                        tt(R("d1"), R("cdi", 384, 512), R("d2"), Op.subtract)
+                        ts(R("wcl"), R("q4", 0, 384), -128 * OFF, Op.add)
+                        for i in range(3):
+                            tt(B("es", i), B("cf", i), B("nio", 0), Op.is_equal)
+                most(k, 3)
+                point(1, 0)
+                laterlists2()
+                conv(1, 0)
+                point(1, 1)
+            elif k < K - 1:
+                most(k, 0)
+                conv(k, 1)
+                point(k + 1, 0)
+                most(k, 1)
+                most(k, 2)
+                conv(k + 1, 0)
+                point(k + 1, 1)
+                if t == 0 and k < 8:
+                    widen(*(("SUM", 1.0), ("SUMH", -0.5), ("SUMK", 16384.0), ("SUMN", -8192.0), ("SWW", C(16)), ("R0", C(17)), ("R1", C(18)))[k - 1])
+                if k == 1:
+                    for s in range(2):
+                        for i in range(3):
+                            mm(B("q%d" % (2 + s), i), [(ID(1.0), B("hc", i)), (ID(1.0), B("lc", i)), (ID(-1.0), B("hb", s)), (ID(-1.0), B("lb", s))])
+                if k in (4, 6):
+                    act(B("eq", k // 5, 384), R("q%d" % (2 + k // 5), 0, 384), AF.Abs)
+                if k in (5, 7):
+                    act(B("ep", k // 6, 384), B("eq", k // 6, 384), AF.Relu, 1.0, -1.0)
+                if t == 0 and k == 8:
+                    act(R("kcol"), R("nio", 0, 16), AF.Identity, 0.5 - OFF)
+                    act(R("blkf"), R("blkm"), AF.Identity, 0.0, C(20))
+                    act(R("lz"), R("lc"), AF.Identity, -OFF)
+                most(k, 3)
+            else:
+                for j in range(4):
+                    for h in range(2):
+                        gat("v", B("EA", 4 * h + j, 512), R("EB"), B("pl1", 4 * h + j, 32), B("EC", 4 * h + j, 512), Op.max)
+                        if j % 2:
+                            i = 2 * h + j // 2
+                            dma(B("EC", i, 1024), B("EA", i, 1024), "s", "ec%d" % i)
+                        if j == 0 and h == 0:
+                            conv(k, 1)
+                            for i in range(4):
+                                ended(i)
+                    fold1(j)
+                    if j > 0:
+                        fold2(j - 1)
+                    if j > 1:
+                        fold3(j - 2)
+                    if j == 1:
+                        sums(0)
+                    if j == 2:
+                        sums2(0)
+        for j in (0, 2, 1, 3):
+            larger(j)
+        fold2(3)
+        fold3(2)
+        sums(1)
+        fold4(0)
+        sums2(1)
+        fold3(3)
+        act(R("s01"), R("q6", 0, 128))
+        fold4(1)
+        largersum(0)
+        largersum(2)
+        largersum(1)
+        largersum(3)
+        mm(R("q7", 0, 128), wrap("SUM", XW, A, A + L))
+        for h in range(2):
+            tt(B("bf", h), R("q%d" % h, 0, 128), R("s01"), Op.add)
+        hi64(R("hb"), R("bf"))
+        unwrap(HI, R("hb"))
+        tt(R("lb"), R("bf"), R("hb"), Op.subtract)
+        unwrap(LO, R("lb"))
+        hi64(R("hs"), R("q7", 0, 128))
+        tt(R("ls"), R("q7", 0, 128), R("hs"), Op.subtract)
+
+        def back(j):
+            gat("a", B("PA", j, 1024), R("PS", 0, 4096), B("bl", j, 64))
+            mm(B("q%d" % (j // 2), j % 2, 64),
+               [(ID(1.0), B("hb", j, 64)), (ID(1.0), B("lb", j, 64)), (ID(16384.0), B("fr", j, 64))]
+               + ([(ID(-16384.0), B("jb", j, 64))] if t else []) + wrap("TWO", "PA", 1024 * j, 1024 * j + 1024))
+
+        def nearsum(i):
+            mm(R("q%d" % (3 + i), 0, 128),
+               [(ID(1.0), B("cst", 0)), (ID(2.0 ** 26), B("es", i)), (ID(-8192.0), R("hs")), (ID(-8192.0), R("ls"))]
+               + wrap("SUMK", "MC", i * L, i * L + L), True, False)
+        for j in range(6):
+            gat("v", B("MC", j, 1024), R(XW, A, A + L + 16), B("cl", j, 64), B("X", j % 2, 1024), Op.max)
+        nearsum(0)
+        back(0)
+        back(1)
+        nearsum(1)
+        back(2)
+        back(3)
+        for h in range(2):
+            ts(B("fr", h), R("q%d" % h, 0, 128), R("thf", t, t + 1), Op.is_ge)
+        tt(R("fb"), B("fr", 0), B("fr", 1), Op.max)
+        unwrap(CAME, R("fb"))
+        unwrap(HI, R("hs"))
+        unwrap(LO, R("ls"))
+        unwrap(LOW, B("fr", 0), L)
+        mm(R("q2", 0, 128), [(R("blkm"), R("fb"))])
+        mm(R("q7", 0, 128), [(R("utm"), R("fb"))])
+        for s in range(2):
+            for i in range(3):
+                mm(B("q%d" % s, i), [(ID(1.0), B("ep", 3 * s + i)), (ID(-1.0), B("fr", s))])
+        nearsum(2)
+        run("v", [R("one"), R("q2", 0, 128)], [R("cum")],
+            lambda: g.vector.tensor_tensor_scan(T.cum[:], T.one[:], T.q2[:, 0:128], 0.0, Op.mult, Op.add))
+        for q in range(NV, 16):
+            act(B("sg", q), R("cum"), AF.Sign, R("kcol", q, q + 1), -1.0, R("acc", q, q + 1))
+        tt(R("pw", 0, 128), R("cum"), R("q7", 0, 128), Op.subtract)
+        for q in range(NV):
+            ts(B("sw", q), R("cum"), R("kcol", q, q + 1), Op.is_le)
+        for q in range(NV):
+            total(R("acc", q, q + 1), B("sw", q))
+        cp(R("l1", 0, NV), R("acc", 0, NV))
+        cp(R("colb", 0, NV), R("acc", 0, NV))
+        act(R("colb", NV, 16), R("acc", NV, 16), AF.Identity, 64.0, 0.5)
+        for s in range(2):
+            act(B("eq", s, 384), R("q%d" % s, 0, 384), AF.Relu)
+        ts(R("l1", NV, 16), R("acc", NV, 16), 0.5, Op.mult, 64.0, Op.add)
+        gat("v", R("cmp"), R("pw"), R("l1"), R("rk"), Op.is_le)
+        mm(R("q2", 0, 16), [(ID(16.0), R("colb"))] + wrap("SUM", "cmp", 0, 256))
+        ts(R("t1"), R("fr"), FREE + OFF, Op.mult)
+        cp(R("l2"), R("q2", 0, 16))
+        gat("v", R("blk%d" % t), R(XW, A, A + L + 16), R("l2"))
+        order("g", [R("blk%d" % t)], [])
+        rid, pid, _ = topo.addr(nxt)
+        ne = len(topo.engines(core, nxt))
+        g.remote_dma(T[XW][:, 0:A], T["blk%d" % t][:], T.sem["arr%d" % t], T.sem.sent, pid, rid, topo.mask(core, nxt))
+        cnt["sent"] = cnt.get("sent", 0) + ne
+        cnt["arr%d" % t] = ne
+        hist.setdefault(XW, []).append((0, A, None, True, ("arr%d" % t, ne), "r"))
+        gat("a", B("SC", 0, L), R("PS", 0, L), B("wcl", 0))
+        gat("v", B("SC", 1, L), R("PS", 0, L), B("wcl", 1))
+        gat("v", R("SC", 2 * L, 2 * L + 512), R("PS", 0, L), R("wcl", 256, 288))
+        gat("a", R("SC", 2 * L + 512, 3 * L), R("PS", 0, L), R("wcl", 288, 384))
+        if not last:
+            unwrap(OPEN, R("fr"))
+        for i in range(3):
+            mm(R("q%d" % (3 + i), 0, 128), [(ID(2.0 ** 26), B("eq", i)), (ID(2.0 ** 26), B("eq", 3 + i))] + wrap("SWW", "SC", i * L, i * L + L)
+               + ([(ID(1.0), B("cst", i))] if i else []) + [(ID(1.0), B("hc", i)), (ID(1.0), B("lz", i))], False, True)
+        for h in range(2):
+            a, b = 3 * L + 1024 * h, 3 * L + 1024 * h + 1024
+            gat("v", R("MC", a, b), R(XW, 0, A), B("cl", 6 + h, 64), B("X", h, 1024), Op.max)
+            gat("a", R("SC", a, b), R(XW, 0, A), B("cl", 6 + h, 64))
+            mm(B("q6", h, 64),
+               [(ID(1.0), R("cst", 384, 448)), (ID(-2.0 ** 28), B("fb", h, 64)), (ID(-8192.0), B("hs", h, 64)), (ID(-8192.0), B("ls", h, 64))]
+               + wrap("SUMN", "SC", a, b) + wrap("SUMK", "MC", a, b) + [(ID(1.0), R("cst", 512, 576))])
+        if not last:
+            mm(R("q1", 0, 256), [(ID(1.0), R("c")), (ID(1.0), R("fr"))])
+            act(R("c"), R("q1", 0, 256), AF.Sign)
+            unwrap(CAME, R("c"))
+        cp(R("km"), R("q3", 0, 128))
+        tt(R("km"), R("km"), R("q4", 0, 128), Op.min)
+        tt(R("ki"), R("km"), R("q5", 0, 128), Op.min)
+        ts(R("ti"), R("ki"), 2047, Op.bitwise_and)
+        tt(R("mix"), R("q6", 0, 128), R("ki"), Op.is_lt)
+        unwrap(MIX, R("mix"), L)
+        ts(R("tq"), R("ti"), OFF, Op.add)
+        hi16(R("hw"), R("tq"))
+        unwrap(HI, R("hw"), L)
+        tt(R("lw"), R("tq"), R("hw"), Op.subtract)
+        unwrap(LO, R("lw"), L)
+        mm(R("q7", 0, 128), [(ID(1.0), B("r16", 0)), (ID(-8192.0), B("fr", 0)), (ID(8192.0), R("mix"))])
+        mm(R("q7", 128, 256), [(ID(1.0), B("r16", 0)), (ID(-8192.0), B("fr", 1)), (ID(8192.0), B("fr", 0)), (ID(8192.0), R("mix"))])
+        mm(R("q2", 0, 128), [(ID(128.0), R("lw")), (ID(0.0625), R("hw"))])
+        act(R("wa"), R("q7", 0, 256), AF.Identity, C(19))
+        tt(R("ml32"), R("d1"), R("mix"), Op.mult)
+        ts(R("tl"), R("q2", 0, 128), -128 * OFF, Op.add)
+        tt(R("ml32"), R("ml32"), R("d2"), Op.add)
+        ts(R("to"), R("ti"), -float(FREE), Op.add)
+        cp(R("ml"), R("ml32"))
+
+        def mixing(j):
+            mm(R("q%d" % (2 + j)), [(ID(0.5), R("mh")), (ID(0.5), B("X", j, 512)), (ID(0.5), B("ab", j, 512))])
+
+        def rounding(j):
+            ts(B("X", j, 512), R("q%d" % (2 + j)), M1, Op.add, M1, Op.subtract)
+
+        def blend(h):
+            gat("a", B("ab", h, 1024), R(XW, 0, A + L), B("ml", h, 64))
+
+        def joined():
+            for h in range(2):
+                tt(B("jb", h), R("q0", 0, 128), B("wa", h), Op.is_equal)
+            if not last:
+                unwrap(JOIN, R("jb"))
+            for h in range(2):
+                tt(B("jj", h), B("jb", h), R("to"), Op.mult)
+            tt(R("m"), R("m"), R("jj"), Op.add)
+        if last:
+            blend(0)
+            mixing(0)
+            mixing(1)
+        gat("v", B("PA", 0, 1024), R("PS", L, 2 * L), B("tl", 0, 64))
+        gat("a", B("PA", 1, 1024), R("PS", L, 2 * L), B("tl", 1, 64))
+        mm(R("q0", 0, 128), wrap("R0", "PA", 0, L))
+        tt(R("m"), R("m"), R("t1"), Op.max)
+        if last:
+            blend(1)
+            mixing(2)
+            mixing(3)
+            rounding(0)
+            rounding(1)
+            dma(T.yx[:, 0:1024], B("X", 0, 1024))
+            joined()
+            ts(R("yo"), R("m"), -OFF, Op.add, 2048.0, Op.min)
+            dma(T.yn[:], R("yo"))
+            rounding(2)
+            rounding(3)
+            dma(T.yx[:, 1024:L], B("X", 1, 1024), "a")
+        else:
+            mm(R("q1", 0, 128), wrap("R1", "PA", 0, L))
+            blend(0)
+            blend(1)
+            joined()
+            hi16(R("hb"), R("m"))
+            unwrap(HI, R("hb"))
+            for h in range(2):
+                tt(B("e0", h), R("q1", 0, 128), B("wa", h), Op.is_equal)
+            unwrap(LESS, R("e0"))
+            tt(R("lb"), R("m"), R("hb"), Op.subtract)
+            unwrap(LO, R("lb"))
+            mixing(0)
+            mixing(1)
+            steplist(1)
+            mixing(2)
+            mixing(3)
+            for j in range(4):
+                rounding(j)
+            cp(R("EA", 0, L), R("X"))
+            cp(R("EA", L, 2 * L), R("X"))
+    for s, n in cnt.items():
+        if n:
+            wait("g", (s, n))

@@ -8,16 +8,23 @@ FREE = 2063
 END = FREE + L
 OFF = 16.25
 C16A, C16B = 2.0 ** 27 - 8, 2.0 ** 27 + 16
-M64 = 805306368.0
 M1 = 12582912.0
 HALF = 0.5 - 2.0 ** -11
+YO = L + 16
 BF, F, I, U = "bfloat16", "float32", "int32", "uint16"
-WN = ["TWO", "PTR", "SUM", "SUMH", "SUMK", "SUMN", "SWW", "R0", "R1"]
-IDS = [256.0, 0.0625, 3968.0, 128.0, -128.0, 1.0, 2048.0, -2048.0, -1.0, 8192.0, -8192.0, 16384.0, -16384.0, 16.0, 0.5,
-       2.0 ** 26, -2.0 ** 28]
-CST = [3 * 2.0 ** 24, 2048.0, 4096.0, 15 * 2.0 ** 24, 6144.0]
-NV = 5
-HI, LO, CAME, LESS, OPEN, LOW, MIX, JOIN = range(8)
+HI, LO, CAME, OPEN, JOIN, JH, JL, CH, CL, CC = range(10)
+W0 = 12
+FRE, LOW, MIX = 2, 3, 4
+SC0, TO0 = 2 * L, 3 * L
+ROWS = {"WTWO": {W0: 1.0, W0 + 1: 1.0},
+        "PTR": {HI: 1.0, LO: 1.0, CAME: 2048.0, JH: -1.0, JL: -1.0, CH: 1.0, CL: 1.0, CC: 2048.0},
+        "TWO": {HI: 1.0, LO: 1.0}, "SWW": {HI: -8192.0, LO: -8192.0, FRE: -2.0 ** 26},
+        "R0": {HI: 1.0, LO: 1.0, MIX: 4096.0}, "R1": {LOW: -2048.0}, "ROW0": {0: 1.0}}
+EVEN = {"FOUR": (W0, 1.0), "SUM": (0, 1.0), "SUMH": (0, -0.5), "SUMK": (0, 16384.0), "SUMN": (0, -8192.0)}
+WN = list(ROWS) + list(EVEN)
+IDS = [128.0, 0.0625, 1920.0, -1.0, 1.0, 15.0, 256.0, -64.0, 992.0, 2048.0, 16384.0, -16384.0, 2.0 ** 26, -8192.0,
+       8192.0, -2.0 ** 28, 16.0, 0.5, 31.25, -16.25, 4096.0, float(YO), -256.0, -0.0625, 8.0]
+CST = [3 * 2.0 ** 24, 2048.0, 15 * 2.0 ** 24, 6144.0]
 
 SCRATCH = {
     "nbi": ("sbuf", [128, 256], I), "cdi": ("sbuf", [128, 512], I), "thi": ("sbuf", [128, 2], I),
@@ -25,43 +32,44 @@ SCRATCH = {
     "X": ("sbuf", [128, L], BF), "EA": ("sbuf", [128, 4112], BF), "EB": ("sbuf", [128, 4112], BF),
     "EC": ("sbuf", [128, 4096], BF),
     "PA": ("sbuf", [128, 4112], BF), "PB": ("sbuf", [128, 4112], BF), "PS": ("sbuf", [128, 4112], BF),
-    "XW0": ("sbuf", [128, A + L + 16], BF), "XW1": ("sbuf", [128, A + L + 16], BF),
+    "PT": ("sbuf", [128, 4 * L], BF),
+    "XW0": ("sbuf", [128, A + YO + L], BF), "XW1": ("sbuf", [128, A + YO + L], BF),
     "blk0": ("sbuf", [128, A], BF), "blk1": ("sbuf", [128, A], BF),
-    "ab": ("sbuf", [128, L], BF), "rr": ("sbuf", [128, L], BF), "rg": ("sbuf", [128, L], BF), "y32": ("sbuf", [128, L], F),
+    "ab": ("sbuf", [128, L], BF), "rr": ("sbuf", [128, L], BF), "y32": ("sbuf", [128, L], F),
     "MC": ("sbuf", [128, 4 * L], BF), "SC": ("sbuf", [128, 4 * L], BF),
-    "wide": ("sbuf", [128, 144 * len(WN)], BF), "idm": ("sbuf", [128, 128 * len(IDS)], BF),
+    "wide": ("sbuf", [128, 144 * len(WN)], BF), "idm": ("sbuf", [128, 128 * len(IDS)], BF), "idf": ("sbuf", [128, 128], F),
     "blkm": ("sbuf", [128, 128], BF), "utm": ("sbuf", [128, 128], BF), "zer": ("sbuf", [128, 128], BF),
     "blkf": ("sbuf", [128, 128], BF), "oneb": ("sbuf", [128, 128], BF),
     "cst": ("sbuf", [128, 128 * len(CST)], BF), "mh": ("sbuf", [128, 512], BF),
-    "pi": ("sbuf", [128, 4], I), "col": ("sbuf", [128, 32], F), "b9": ("sbuf", [128, 16], F),
+    "pi": ("sbuf", [128, 4], I), "col": ("sbuf", [128, 16], F), "ew": ("sbuf", [128, 16], F),
     "rk": ("sbuf", [128, 256], F), "r16": ("sbuf", [128, 256], BF),
     "nio": ("sbuf", [128, 256], F), "kcol": ("sbuf", [128, 16], F),
-    "m": ("sbuf", [128, 256], F), "c": ("sbuf", [128, 256], BF), "fr": ("sbuf", [128, 256], BF),
-    "hb": ("sbuf", [128, 256], BF), "lb": ("sbuf", [128, 256], BF), "l0": ("sbuf", [128, 256], BF),
+    "lk": ("sbuf", [128, 768], BF), "ct": ("sbuf", [128, 768], BF), "jn": ("sbuf", [128, 768], BF),
+    "fr": ("sbuf", [128, 256], BF), "jb": ("sbuf", [128, 256], BF), "sq": ("sbuf", [128, 256], BF),
+    "l0": ("sbuf", [128, 256], BF), "bh": ("sbuf", [128, 256], BF), "bo": ("sbuf", [128, 256], BF),
     "hs": ("sbuf", [128, 128], BF), "ls": ("sbuf", [128, 128], BF),
     "hw": ("sbuf", [128, 128], BF), "lw": ("sbuf", [128, 128], BF),
     "t1": ("sbuf", [128, 256], F), "t2": ("sbuf", [128, 256], F), "nn": ("sbuf", [128, 256], F),
-    "bf": ("sbuf", [128, 256], F), "s01": ("sbuf", [128, 128], F),
-    "wl": ("sbuf", [128, 256], U), "sl": ("sbuf", [128, 256], U), "bl": ("sbuf", [128, 256], U),
+    "s01": ("sbuf", [128, 128], F),
+    "wl": ("sbuf", [128, 256], U), "el": ("sbuf", [128, 256], U), "sl": ("sbuf", [128, 256], U), "bl": ("sbuf", [128, 256], U),
     "pl0": ("sbuf", [128, 256], U), "pl1": ("sbuf", [128, 256], U),
     "cl": ("sbuf", [128, 512], U), "wcl": ("sbuf", [128, 384], U), "cf": ("sbuf", [128, 384], F),
     "hc": ("sbuf", [128, 384], BF), "lc": ("sbuf", [128, 384], BF), "lz": ("sbuf", [128, 384], BF),
     "es": ("sbuf", [128, 384], BF), "eq": ("sbuf", [128, 768], BF), "ep": ("sbuf", [128, 768], BF),
-    "sw": ("sbuf", [128, 128 * NV], F),
-    "d1": ("sbuf", [128, 128], F), "d2": ("sbuf", [128, 128], F), "ml32": ("sbuf", [128, 128], F),
+    "sw": ("sbuf", [128, 128], F), "upto": ("sbuf", [128, 128], F), "cumb": ("sbuf", [128, 128], BF),
     "fb": ("sbuf", [128, 128], BF), "cum": ("sbuf", [128, 128], F), "pw": ("sbuf", [128, 144], F),
-    "one": ("sbuf", [128, 128], F), "sg": ("sbuf", [128, 2048], BF), "acc": ("sbuf", [128, 16], F),
-    "colb": ("sbuf", [128, 16], BF), "l1": ("sbuf", [128, 16], U), "l2": ("sbuf", [128, 16], U),
-    "cmp": ("sbuf", [128, 256], BF),
+    "one": ("sbuf", [128, 128], F), "tab": ("sbuf", [128, 32], F), "rkb": ("sbuf", [128, 256], BF),
+    "colb": ("sbuf", [128, 32], BF), "l1": ("sbuf", [128, 32], U), "l2": ("sbuf", [128, 16], U),
+    "cmp": ("sbuf", [128, 768], BF),
     "km": ("sbuf", [128, 128], F), "ki": ("sbuf", [128, 128], I), "ti": ("sbuf", [128, 128], I),
-    "tq": ("sbuf", [128, 128], F), "to": ("sbuf", [128, 128], F), "tl": ("sbuf", [128, 128], U),
+    "tq": ("sbuf", [128, 128], F), "tl": ("sbuf", [128, 128], U),
     "ml": ("sbuf", [128, 128], U), "mix": ("sbuf", [128, 128], BF),
-    "wa": ("sbuf", [128, 256], F), "jb": ("sbuf", [128, 256], BF), "jj": ("sbuf", [128, 256], F),
-    "e0": ("sbuf", [128, 256], BF), "yo": ("sbuf", [128, 256], F),
+    "wa": ("sbuf", [128, 256], F), "jj": ("sbuf", [128, 256], F), "yo": ("sbuf", [128, 256], F),
 }
 for _b in range(8):
     SCRATCH["q%d" % _b] = ("psum", [128, 512], F)
-NDMA = 48
+LOOSE, SLACK, MARGIN, WAKE, GATHER = {"p": 30, "s": 12, "a": 30, "v": 30, "g": 1}, 0.1, 0.4, 0.1, 1.5
+NDMA = 72
 SEMAPHORES = (["sv", "sa", "sp", "sg", "sent"] + ["arr%d" % t for t in range(RO)] + ["ec%d" % i for i in range(4)]
               + ["dm%d" % i for i in range(NDMA)])
 
@@ -77,13 +85,14 @@ def rank_program(g, core, T, topo):
     clock = {}
     hist = {}
     ndma = [0]
+    todo, done = [], {}
 
     def R(name, a=0, b=None, step=1, row=None):
         t = T[name]
         if b is None:
             b = t.shape[1]
         cs = slice(a, b) if step == 1 else slice(a, b, step)
-        return (t[:, cs] if row is None else t[row::16, cs], name, a, b, row)
+        return (t[:, cs] if row is None else t[row::16, cs], name, a, b, row, len(range(a, b, step)))
 
     def B(name, i, n=128):
         return R(name, n * i, n * i + n)
@@ -104,90 +113,162 @@ def rank_program(g, core, T, topo):
             for r in lst:
                 ps = r[1][0] == "q"
                 for a, b, row, w2, tok, e2 in hist.get(r[1], []):
+                    apart = b <= r[2] or r[3] <= a
                     if ps:
-                        if e2 == e and ((e == "p" and cont) or not (w or w2)):
+                        if e2 == e and (cont or apart or not (w or w2)):
                             continue
-                    elif not (w or w2) or b <= r[2] or r[3] <= a or (row is not None and r[4] is not None and row != r[4]):
+                    elif not (w or w2) or apart or (row is not None and r[4] is not None and row != r[4]):
                         continue
                     need[tok[0]] = max(need.get(tok[0], 0), tok[1])
         for s, n in need.items():
-            wait(e, (s, n))
+            if not any(clock.get(tok, {}).get(s, 0) >= n for tok in need.items()):
+                wait(e, (s, n))
 
     def note(e, tok, reads, writes):
         clock[tok] = dict(known[e])
         for lst, w in ((reads, False), (writes, True)):
             for r in lst:
                 h = hist.setdefault(r[1], [])
-                if w:
-                    h[:] = [x for x in h if not (r[1][0] == "q" or (r[2] <= x[0] and x[1] <= r[3] and (r[4] is None or r[4] == x[2])))]
+                if r[1][0] == "q":
+                    h[:] = [x for x in h if x[5] == e and not (w and r[2] <= x[0] and x[1] <= r[3])]
+                elif w:
+                    h[:] = [x for x in h if not (r[2] <= x[0] and x[1] <= r[3] and (r[4] is None or r[4] == x[2]))]
                 h.append((r[2], r[3], r[4], w, tok, e))
 
-    def run(e, reads, writes, call, cont=False):
-        reads = [r for r in reads if isinstance(r, tuple)]
+    def issue(e, reads, writes, call, cont, kind):
         order(e, reads, writes, cont)
-        s = "s" + e
-        cnt[s] += 1
-        call().then_inc(T.sem[s], 1)
+        if kind == "remote":
+            return call()
+        s, n = "s" + e, 1
+        if kind != "compute":
+            s, n = kind, 16
+            if kind == "dma":
+                s = "dm%d" % ndma[0]
+                ndma[0] += 1
+            elif cnt.get(s):
+                wait(e, (s, cnt[s]))
+        cnt[s] = cnt.get(s, 0) + n
+        call().then_inc(T.sem[s], n)
         note(e, (s, cnt[s]), reads, writes)
+
+    def run(e, reads, writes, call, cost, late=0.0, cont=False, kind="compute"):
+        todo.append((e, [r for r in reads if isinstance(r, tuple)], writes, call, cont, kind, cost, late))
+
+    def schedule():
+        seen, before, tail = {}, [], {}
+        for i, (e, reads, writes, *_) in enumerate(todo):
+            d = set()
+            for lst, w in ((reads, False), (writes, True)):
+                for r in lst:
+                    for a, b, row, w2, j in seen.get(r[1], []):
+                        if r[1][0] == "q" or ((w or w2) and a < r[3] and r[2] < b and (row is None or r[4] is None or row == r[4])):
+                            d.add(j)
+            for lst, w in ((reads, False), (writes, True)):
+                for r in lst:
+                    h = seen.setdefault(r[1], [])
+                    if r[1][0] == "q":
+                        h[:] = []
+                    elif w:
+                        h[:] = [x for x in h if not (r[2] <= x[0] and x[1] <= r[3] and (r[4] is None or r[4] == x[2]))]
+                    h.append((r[2], r[3], r[4], w, i))
+            d.discard(i)
+            before.append(d)
+            tail.setdefault(e, []).append(i)
+        free = {e: 0.0 for e in Q}
+
+        def soonest(i, memo):
+            if i not in memo:
+                memo[i] = max([free[todo[i][0]]] + [done[j] if j in done else soonest(j, memo) + todo[j][6] + todo[j][7] + WAKE for j in before[i]])
+            return memo[i]
+        while len(done) < len(todo):
+            best, memo = None, {}
+            for e, mine in tail.items():
+                limit = 1e9
+                for i in mine[:LOOSE.get(e, 1)]:
+                    t0 = soonest(i, memo)
+                    if t0 + todo[i][6] <= limit + SLACK and all(j in done for j in before[i]) and (best is None or t0 < best[0]):
+                        if i == mine[0] or e in "ps" or all(done[j] + MARGIN <= t0 for j in before[i] if todo[j][0] != e):
+                            best = (t0, i)
+                    limit = min(limit, t0)
+            t0, i = best
+            e, reads, writes, call, cont, kind, cost, late = todo[i]
+            tail[e].remove(i)
+            issue(e, reads, writes, call, cont, kind)
+            free[e] = t0 + cost
+            done[i] = t0 + cost + late + WAKE
 
     def ap(x):
         return x[0] if isinstance(x, tuple) else x
 
-    def dma(out, in_, e="s", s=None):
-        reads = [in_] if isinstance(in_, tuple) else []
-        writes = [out] if isinstance(out, tuple) else []
-        order(e, reads, writes)
-        if s is None:
-            s = "dm%d" % ndma[0]
-            ndma[0] += 1
-        elif cnt.get(s):
-            wait(e, (s, cnt[s]))
-        Q[e].dma_start(ap(out), ap(in_)).then_inc(T.sem[s], 16)
-        cnt[s] = cnt.get(s, 0) + 16
-        note(e, (s, cnt[s]), reads, writes)
+    def us(n, *sides, fix=0.0):
+        if sides and all(SCRATCH[x[1]][2] in (BF, U) for x in sides):
+            n = n / 2
+        return fix + max(n, 64) * 1e-3
 
-    def unwrap(row, src, a=0):
-        dma(R("PS", a, a + 16 * (src[3] - src[2]), row=row), src)
+    def dma(out, in_, e="s", s="dma", after=None):
+        sb = in_ if isinstance(in_, tuple) else out
+        size = sb[5] * (2 if SCRATCH[sb[1]][2] == BF else 4)
+        run(e, [in_, after], [out] if isinstance(out, tuple) else [], lambda: Q[e].dma_start(ap(out), ap(in_)), 0.05, 1.5 + size * 4e-4, kind=s)
+
+    def unwrap(win, row, src, a=0):
+        dma(R(win, a, a + 16 * (src[3] - src[2]), row=row), src)
 
     def ts(out, in0, s1, op0, s2=None, op1=None):
         if op1 is None:
-            run("v", [in0, s1], [out], lambda: g.vector.tensor_scalar(out[0], in0[0], ap(s1), None, op0))
+            run("v", [in0, s1], [out], lambda: g.vector.tensor_scalar(out[0], in0[0], ap(s1), None, op0), us(out[5], out, in0))
         else:
-            run("v", [in0, s1, s2], [out], lambda: g.vector.tensor_scalar(out[0], in0[0], ap(s1), ap(s2), op0, op1))
+            run("v", [in0, s1, s2], [out], lambda: g.vector.tensor_scalar(out[0], in0[0], ap(s1), ap(s2), op0, op1), us(out[5], out, in0))
 
     def tt(out, in0, in1, op):
-        run("v", [in0, in1], [out], lambda: g.vector.tensor_tensor(out[0], in0[0], in1[0], op))
+        run("v", [in0, in1], [out], lambda: g.vector.tensor_tensor(out[0], in0[0], in1[0], op), us(out[5] * (1 if in0[1][0] == "q" else 2)))
 
     def cp(out, in_):
-        run("v", [in_], [out], lambda: g.vector.tensor_copy(out[0], in_[0]))
+        run("v", [in_], [out], lambda: g.vector.tensor_copy(out[0], in_[0]), us(out[5], out, in_))
 
-    def total(out, in_):
-        run("v", [in_], [out], lambda: g.vector.tensor_reduce(out[0], in_[0], AX.X, Op.add))
+    def total(out, in_, op=Op.add):
+        run("v", [in_], [out], lambda: g.vector.tensor_reduce(out[0], in_[0], AX.X, op), us(in_[5]))
 
     def fill(out, val):
-        run("v", [], [out], lambda: g.vector.memset(out[0], val))
+        run("v", [], [out], lambda: g.vector.memset(out[0], val), us(out[5], out))
 
     def act(out, in_, func=AF.Identity, bias=0.0, scale=1.0, accum=None):
         w = [out] + ([accum] if accum else [])
         if accum:
-            run("a", [in_, bias, scale], w, lambda: g.scalar.activation(out[0], in_[0], func, ap(bias), ap(scale), accum_out=accum[0]))
+            run("a", [in_, bias, scale], w, lambda: g.scalar.activation(out[0], in_[0], func, ap(bias), ap(scale), accum_out=accum[0]), us(out[5], fix=0.08))
         else:
-            run("a", [in_, bias, scale], w, lambda: g.scalar.activation(out[0], in_[0], func, ap(bias), ap(scale)))
+            run("a", [in_, bias, scale], w, lambda: g.scalar.activation(out[0], in_[0], func, ap(bias), ap(scale)), us(out[5], fix=0.065))
 
     def gat(e, out, win, off, in1=None, op=None):
+        c = us(GATHER * out[5], fix=0.06)
         if e == "a":
-            run("a", [win, off], [out], lambda: g.scalar.activation(out[0], win[0].indirect(off[0]), AF.Copy))
+            run("a", [win, off], [out], lambda: g.scalar.activation(out[0], win[0].indirect(off[0]), AF.Copy), c)
         elif in1 is None:
-            run("v", [win, off], [out], lambda: g.vector.tensor_copy(out[0], win[0].indirect(off[0])))
+            run("v", [win, off], [out], lambda: g.vector.tensor_copy(out[0], win[0].indirect(off[0])), c)
         else:
-            run("v", [win, off, in1], [out], lambda: g.vector.tensor_tensor(out[0], win[0].indirect(off[0]), in1[0], op))
+            run("v", [win, off, in1], [out], lambda: g.vector.tensor_tensor(out[0], win[0].indirect(off[0]), in1[0], op), c)
+
+    def mms(terms, start=True, stop=True):
+        def call():
+            for i, (o, l, r) in enumerate(terms):
+                ins = g.tensor.matmul(o[0], l[0], r[0], start and i == 0, stop and i == len(terms) - 1)
+            return ins
+        cost = sum(max(64, r[5]) * (4 if SCRATCH[r[1]][2] == F else 1) for o, l, r in terms) * 5e-4
+        run("p", [x for t in terms for x in t[1:]], list({t[0][1:]: t[0] for t in terms}.values()), call, cost, cont=not start)
 
     def mm(out, terms, start=True, stop=True):
+        mms([(out, l, r) for l, r in terms], start, stop)
+
+    def send(t):
+        rid, pid, _ = topo.addr(nxt)
+        ne = len(topo.engines(core, nxt))
+        land = R("XW%d" % t, 0, A)
+
         def call():
-            for i, (l, r) in enumerate(terms):
-                ins = g.tensor.matmul(out[0], l[0], r[0], start and i == 0, stop and i == len(terms) - 1)
-            return ins
-        run("p", [x for t in terms for x in t], [out], call, cont=not start)
+            g.remote_dma(land[0], T["blk%d" % t][:], T.sem["arr%d" % t], T.sem.sent, pid, rid, topo.mask(core, nxt))
+            cnt["sent"] = cnt.get("sent", 0) + ne
+            cnt["arr%d" % t] = ne
+            hist.setdefault(land[1], []).append((0, A, None, True, ("arr%d" % t, ne), "r"))
+        run("g", [R("blk%d" % t)], [land], call, 0.1, 3.5, kind="remote")
 
     def wrap(w, name, a, b):
         o = 144 * WN.index(w)
@@ -195,421 +276,557 @@ def rank_program(g, core, T, topo):
 
     def iota(out, pattern, base, cm, flt=True):
         if flt:
-            run("g", [], [out], lambda: g.iota(out[0], pattern, base, cm, allow_small_or_imprecise_dtypes=True))
+            run("g", [], [out], lambda: g.iota(out[0], pattern, base, cm, allow_small_or_imprecise_dtypes=True), us(2 * out[5], fix=0.13))
         else:
-            run("g", [], [out], lambda: g.iota(out[0], pattern, base, cm))
+            run("g", [], [out], lambda: g.iota(out[0], pattern, base, cm), us(2 * out[5], fix=0.13))
 
     def select(out, in_, pattern, op, val, base, cm):
-        run("g", [in_], [out], lambda: g.affine_select(out[0], in_[0], pattern, op, val, base, cm))
+        run("g", [in_], [out], lambda: g.affine_select(out[0], in_[0], pattern, op, val, base, cm), us(2 * out[5], fix=0.17))
+
+    def gcopy(out, in_):
+        select(out, in_, [[0, out[5]]], Op.is_ge, 0.0, 0, 0)
 
     def ID(val):
         return B("idm", IDS.index(val))
 
+    def ident(*vals):
+        return [(ID(val), R("zer"), [[-1, 128]], Op.not_equal, val, 0, 1) for val in vals]
+
+    def by_row(out, rows, pattern=((-16, 8),)):
+        return [(out, out, [list(p) for p in pattern], Op.not_equal, val, -r, 1) for r, val in rows.items()]
+
+    def weights(w, rows=None):
+        o = 144 * WN.index(w)
+        out = R("wide", o + 15, o + 143, 16)
+        if w in ROWS:
+            return by_row(out, {r: v for r, v in ROWS[w].items() if rows is None or r in rows})
+        return [(out, out, [[16, 8]], Op.is_gt, EVEN[w][1], EVEN[w][0], -1), (out, out, [[16, 8]], Op.is_ge, 0.0, 15, -1)]
+
+    def weave(*chains):
+        for i in range(max(len(c) for c in chains)):
+            for c in chains:
+                if i < len(c):
+                    (select if len(c[i]) == 7 else iota)(*c[i])
+
+    def zero(*outs):
+        return [(o, [[0, o[5]]], 0, 0) for o in outs]
+
     def C(k):
         return R("col", k, k + 1)
-
-    def ROW(r):
-        return C(3 + r)
 
     def hi16(h, src):
         ts(h, src, C16A, Op.add, C16B, Op.subtract)
 
-    def hi64(h, src):
-        ts(h, src, M64, Op.add, M64, Op.subtract)
+    hb, lb, cc = B("lk", 0, 256), B("lk", 1, 256), B("lk", 2, 256)
 
-    def widen(w, scale):
-        o = 144 * WN.index(w)
-        act(R("wide", o + 15, o + 144, 16), R("b9", 0, 9), AF.Identity, 0.0, scale)
+    def H(x, h, n=128):
+        return R(x[1], x[2] + n * h, x[2] + n * h + n)
 
-    def steplist(t):
-        mm(R("q6", 0, 256), [(ID(256.0), R("lb")), (ID(0.0625), R("hb")), (ID(128.0), R("c"))] + ([(ID(-128.0), R("e0"))] if t else []))
-        ts(R("wl"), R("q6", 0, 256), -256 * OFF, Op.add)
+    def laterlists(bank):
+        act(R("sq"), hb, AF.Sign, -1016.0)
+        mm(R(bank, 0, 256), [(ID(128.0), lb), (ID(0.0625), hb), (ID(-64.0), cc), (ID(992.0), R("sq"))])
+        mm(R(bank, 256, 512), [(ID(1.0), lb), (ID(1.0), hb), (ID(2048.0), cc)])
 
-    def laterlists(t):
-        mm(R("q7", 0, 256), [(ID(256.0), R("lb")), (ID(0.0625), R("hb")), (ID(-128.0), R("c"))] + ([(ID(128.0), R("e0"))] if t else []))
-        mm(R("q6", 256, 512), [(ID(1.0), R("lb")), (ID(1.0), R("hb")), (ID(2048.0), R("c"))] + ([(ID(-2048.0), R("e0"))] if t else []))
+    def laterlists2(bank):
+        ts(R("bl"), R(bank, 0, 256), 64 + 992 - 128 * OFF, Op.add)
+        ts(R("sl"), R(bank, 256, 512), -OFF, Op.add)
 
-    def laterlists2():
-        ts(R("bl"), R("q7", 0, 256), 128 - 256 * OFF, Op.add)
-        ts(R("sl"), R("q6", 256, 512), -OFF, Op.add)
+    def near(s):
+        mm(R("q%d" % s, 0, 384), [(ID(1.0), R("hc")), (ID(1.0), R("lc"))], True, False)
+        mms([(B("q%d" % s, i), ID(-1.0), H(x, s)) for i in range(3) for x in (hb, lb)], False, True)
+
+    def near2(s):
+        act(B("eq", s, 384), R("q%d" % s, 0, 384), AF.Abs, -2064.0)
+
+    def near3(s):
+        act(B("ep", s, 384), B("eq", s, 384), AF.Relu, 1.0, -1.0)
 
     dma(R("nbi"), T.nb[:])
-    dma(R("cdi"), T.cd[:], "a")
-    dma(R("thi"), T.th[:], "a")
-    dma(R("X"), T.x0[:], "a")
+    dma(R("cdi"), T.cd[:])
+    fill(R("PS", 0, L + 16), 0.0)
     iota(R("pi", 0, 1), [[0, 1]], 0, 1, False)
-    iota(R("b9"), [[1, 16]], 0, 0)
+    iota(R("ew"), [[0, 16]], 0, 0)
     iota(R("zer"), [[0, 128]], 0, 0)
-    for val in IDS[:3]:
-        select(ID(val), R("zer"), [[-1, 128]], Op.not_equal, val, 0, 1)
-    iota(R("r16"), [[0, 2], [16, 128]], 0, 0)
-    for val in IDS[3:]:
-        select(ID(val), R("zer"), [[-1, 128]], Op.not_equal, val, 0, 1)
-    for w in ("EA", "EB", "PA", "PB"):
-        iota(R(w, 4096, 4112), [[0, 16]], 0, 0)
-    iota(R("rk"), [[1, 256]], 0, 0)
-    iota(R("one"), [[0, 128]], 1, 0)
-    iota(R("oneb"), [[0, 128]], 1, 0)
-    select(R("utm"), R("oneb"), [[-16, 8], [0, 16]], Op.is_ge, 0.0, 0, 1)
-    select(R("blkm"), R("utm"), [[16, 8], [0, 16]], Op.is_ge, 0.0, 15, -1)
-    select(R("utm"), R("blkm"), [[-1, 128]], Op.is_gt, 0.0, 0, 1)
-    for i, val in enumerate(CST):
-        select(B("cst", i), R("zer"), [[0, 128]], Op.is_gt, val, 0, 0)
-    for j in range(4):
-        select(B("mh", j), R("zer"), [[0, 128]], Op.is_gt, -0.5, 0, 0)
-    iota(R("pw", 128, 144), [[0, 16]], 65536, 0)
-    for t in range(RO):
-        iota(R("XW%d" % t, A + L, A + L + 16), [[0, 16]], 0, 0)
-    fill(R("PS", 0, L), 0.0)
-    act(R("PS", L, 2 * L), R("PS", 0, L), AF.Copy)
-    ts(R("pi", 1, 2), R("pi", 0, 1), 15, Op.bitwise_and)
-    ts(R("pi", 2, 3), R("pi", 0, 1), 4, Op.arith_shift_right)
-    fill(R("PS", 2 * L, 4112), 0.0)
-    cp(R("col", 0, 3), R("pi", 0, 3))
+    act(R("PS", L + 16, 4112), R("PS", 0, L), AF.Copy)
     fill(R("wide"), 0.0)
-    ts(R("col", 3, 11), R("b9", 0, 8), C(1), Op.is_equal)
-    ts(C(11), C(1), 1.0, Op.is_le)
+    weave(by_row(R("ew", 0, 8), {W0: 2048.0, W0 + 1: 15 + OFF, W0 + 2: 4096.0}), ident(*IDS[:3]))
+    ts(R("pi", 1, 2), R("pi", 0, 1), 15, Op.bitwise_and)
+    total(R("PS", L, L + 1), R("ew", 0, 8), Op.max)
+    cp(C(1), R("pi", 1, 2))
+    iota(R("r16"), [[0, 2], [16, 128]], 0, 0)
+    select(R("idf"), R("zer"), [[-1, 128]], Op.not_equal, 1.0, 0, 1)
+    weave(weights("WTWO"), weights("FOUR"), ident(*IDS[3:7]))
+    weave(by_row(R("ew", 8, 16), {HI: 2048.0, LO: 15 + OFF, CAME: 1.0, OPEN: 1.0}), weights("PTR", (HI, LO, CAME)),
+          zero(R("EA", L, L + 16), *[R(w, 4096, 4112) for w in ("PA", "PB", "EA", "EB")]))
+
+    def constants():
+        weave(ident(*IDS[7:]), [(R("oneb"), [[0, 128]], 1, 0), (R("utm"), R("oneb"), [[-16, 8], [0, 16]], Op.is_ge, 0.0, 0, 1),
+                                (R("blkm"), R("utm"), [[16, 8], [0, 16]], Op.is_ge, 0.0, 15, -1), (R("utm"), [[0, 128]], 0, 0),
+                                (R("utm"), R("utm"), [[1, 128]], Op.is_ge, -1.0, 0, -1), (R("utm"), R("utm"), [[16, 8], [0, 16]], Op.is_ge, 0.0, 15, -1)],
+              zero(R("blkf")) + by_row(R("blkf"), {JOIN: 512.0, OPEN: -512.0}, ((-16, 8), (0, 16))),
+              *[weights(w) for w in WN if w not in ("WTWO", "FOUR", "PTR")])
+        iota(R("rk"), [[1, 256]], 0, 0)
+        iota(R("rkb"), [[1, 256]], 0, 0)
+        iota(R("tab", 16, 32), [[0, 16]], 65536, 0)
+        iota(R("one"), [[0, 128]], 1, 0)
+        for i, val in enumerate(CST):
+            select(B("cst", i), R("zer"), [[0, 128]], Op.is_gt, val, 0, 0)
+        for j in range(4):
+            select(B("mh", j), R("zer"), [[0, 128]], Op.is_gt, -0.5, 0, 0)
+        iota(R("pw", 128, 144), [[0, 16]], 65536, 0)
+        weave(zero(R("XW0", A + L, A + YO), R("XW1", A + L, A + YO), R("PT")))
     ts(R("t1"), R("nbi"), OFF, Op.add)
+    hi16(hb, R("t1"))
+    for s in range(2):
+        unwrap("PS", W0 + 2 * s, H(hb, s))
+    tt(R("l0"), R("t1"), hb, Op.subtract)
+    for s in range(2):
+        unwrap("PS", W0 + 2 * s + 1, B("l0", s))
+    dma(R("EA", 0, L), T.x0[:], after=R("l0"))
+    dma(R("thi"), T.th[:], after=R("l0"))
     ts(R("fr"), R("nbi"), 2048.0, Op.is_ge)
-    hi16(R("hb"), R("t1"))
-    unwrap(HI, R("hb"))
-    ts(R("b9", 0, 9), R("b9", 0, 9), C(2), Op.is_equal)
-    tt(R("l0"), R("t1"), R("hb"), Op.subtract)
-    unwrap(LO, R("l0"))
-    dma(R("EA", 0, L), T.x0[:])
-    dma(R("EA", L, 2 * L), T.x0[:])
-    mm(R("q6", 0, 256), [(ID(256.0), R("l0")), (ID(0.0625), R("hb")), (ID(3968.0), R("fr"))])
-    ts(C(12), ROW(LO), 15 + OFF, Op.mult, ROW(CAME), Op.add)
+    mm(R("q6", 0, 256), [(ID(128.0), R("l0")), (ID(0.0625), hb), (ID(1920.0), R("fr"))])
+    ts(C(2), C(1), OFF, Op.add)
+    ts(C(3), C(1), -1.0, Op.mult, -2 * OFF, Op.add)
     ts(R("t2"), R("fr"), FREE + OFF, Op.mult)
-    ts(C(13), ROW(HI), 2048.0, Op.mult, ROW(OPEN), Op.add)
-    ts(R("wl"), R("q6", 0, 256), -256 * OFF, Op.add)
-    ts(R("PS", 4096, 4097), C(12), C(13), Op.add)
-    widen("TWO", C(11))
-    ts(R("nio"), R("r16"), C(1), Op.add, OFF, Op.add)
+    ts(R("wl"), R("q6", 0, 256), -128 * OFF, Op.add)
+    act(R("nio"), R("r16"), AF.Identity, C(2))
+    ts(R("cf"), R("cdi", 0, 384), 2064 + OFF, Op.add)
     tt(R("nn"), R("t2"), R("nio"), Op.max)
-    for j in (0, 2, 3, 1):
-        gat("va"[j // 2], B("PA", j, 1024), R("PS"), B("wl", j, 64))
-        mm(B("q%d" % (j // 2), j % 2, 64), wrap("TWO", "PA", 1024 * j, 1024 * j + 1024))
-    tt(R("m"), R("t1"), R("t2"), Op.max)
-    unwrap(OPEN, R("fr"))
-    tt(B("c", 1), R("q1", 0, 128), B("nn", 1), Op.is_equal)
-    tt(R("lb"), R("m"), R("hb"), Op.subtract)
-    unwrap(LO, R("lb"))
-    tt(B("c", 0), R("q0", 0, 128), B("nn", 0), Op.is_equal)
-    unwrap(CAME, R("c"))
-    ts(C(14), ROW(CAME), 2048.0, Op.mult, C(11), Op.add)
-    steplist(0)
-    ts(C(14), ROW(LESS), -2048.0, Op.mult, C(14), Op.add)
-    widen("PTR", C(14))
+    act(R("hc"), R("cf"), AF.Identity, -7.5 - OFF)
+    mm(R("q7", 0, 384), [(R("idf"), R("cf")), (ID(-1.0), R("hc"))])
+    mm(R("q5", 0, 256), [(ID(1.0), R("l0")), (ID(15.0), R("fr"))])
+
+    def reach(j):
+        gat("va"[j // 2], B("PB", j, 1024), R("PS", 0, L + 16), B("wl", j, 64))
+
+    def came(j):
+        mm(B("q%d" % (j // 2), j % 2, 64), wrap("WTWO", "PB", 1024 * j, 1024 * j + 1024))
+
+    def twice(j):
+        mm(B("q2", j, 64), [(ID(-1.0), B("r16", j, 64))] + wrap("FOUR", "PB", 1024 * j, 1024 * j + 1024))
+
+    def twice2(a, b):
+        ts(R("el", 64 * a, 64 * b), R("q2", 64 * a, 64 * b), C(3), Op.add, 2048.0, Op.min)
+    for j in (0, 2, 1, 3):
+        reach(j)
+    act(lb, R("q5", 0, 256))
+    came(0)
+    came(2)
+    twice(0)
+    came(3)
+    came(1)
+    mm(R("q6", 0, 256), [(ID(256.0), lb), (ID(0.0625), hb)], True, False)
+    unwrap("PS", HI, hb)
+    unwrap("PS", LO, lb)
+    unwrap("PS", OPEN, R("fr"))
+    total(R("PS", 4096, 4097), R("ew", 8, 16), Op.max)
+    ts(C(4), C(1), 8192 + OFF, Op.add)
+    ts(C(6), C(1), -1.0, Op.mult, -2064 - OFF, Op.add)
+    ts(C(7), C(1), 8.0, Op.is_ge, 65536.0, Op.mult)
+    ts(C(9), C(1), 128.0, Op.mult, 112.0, Op.add)
+    ts(R("upto"), B("r16", 0), C(9), Op.is_le)
+    cp(R("cl"), R("cdi"))
+    twice2(0, 1)
+    tt(H(cc, 1), R("q1", 0, 128), B("nn", 1), Op.is_equal)
+    tt(H(cc, 0), R("q0", 0, 128), B("nn", 0), Op.is_equal)
+    unwrap("PS", CAME, cc)
+    mm(R("q6", 0, 256), [(ID(128.0), cc)], False, True)
+    act(B("X", 0, 1024), B("EA", 0, 1024))
+    act(R("lc"), R("q7", 0, 384))
+    act(R("lz"), R("q7", 0, 384), AF.Identity, -16 - OFF)
     act(R("PA", END, END + 1), R("PS", 4096, 4097), AF.Copy)
     act(R("PB", END, END + 1), R("PS", 4096, 4097), AF.Copy)
-    act(R("d2"), R("nio", 0, 128), AF.Identity, A - OFF)
-    ts(C(15), C(11), -8192.0, Op.mult)
-    ts(C(17), ROW(MIX), 4096.0, Op.mult, C(11), Op.add)
-    ts(C(20), ROW(JOIN), ROW(OPEN), Op.subtract, 512.0, Op.mult)
-    ts(C(16), ROW(CAME), -2.0 ** 26, Op.mult, C(15), Op.add)
-    ts(C(18), ROW(LOW), 0.5, Op.mult, C(17), Op.add)
-    ts(C(19), C(1), 8192 + OFF, Op.add)
-    ts(R("thf"), R("thi"), 0.5, Op.mult)
-    ts(R("cf"), R("cdi", 0, 384), OFF, Op.add)
-    cp(R("cl"), R("cdi"))
-    hi16(R("hc"), R("cf"))
-    tt(R("lc"), R("cf"), R("hc"), Op.subtract)
+    mm(R("q5", 0, 384), [(ID(1.0), R("hc")), (ID(1.0), R("lc"))], True, False)
+    mms([(B("q5", i), ID(-1.0), B("r16", 0)) for i in range(3)], False, True)
+    act(R("es"), R("q5", 0, 384), AF.Abs, C(6))
+    act(R("es"), R("es"), AF.Relu, 1.0, -1.0)
+    for j in (1, 2, 3):
+        twice(j)
+    gcopy(B("X", 1, 1024), B("EA", 1, 1024))
+    constants()
 
     for t in range(RO):
         last = t == RO - 1
         XW = "XW%d" % t
+        XF = R(XW, A, A + YO)
+        FQ, RQ, LQ = ("q6", "q7", "q2", "q0"), ("q4", "q5", "q0", "q1"), ("q5", "q3")
 
-        def point(k, h):
+        def first(e, j):
+            gat(e, B("PA", j, 1024), R("PS"), B("wl", j, 64))
+            mm(bank(0, j), wrap("PTR", "PA", 1024 * j, 1024 * j + 1024))
+
+        def bank(k, j):
+            return R(("q0", "q1", "q3", "q4")[j], 0, 64) if k == 0 else B("q%d" % (turn(k).index(j) % 2), j // 2, 64)
+
+        def point(k, j):
             src, dst = ("PA", "PB")[(k - 1) % 2], ("PA", "PB")[k % 2]
-            gat("a", B(dst, h, L), R(src), B("pl%d" % ((k - 1) % 2), h))
-            mm(R("q%d" % h, 0, 128), wrap("PTR", dst, h * L, h * L + L))
+            gat("a", B(dst, j, 1024), R(src), B("pl%d" % ((k - 1) % 2), j, 64))
+            mm(bank(k, j), wrap("PTR", dst, 1024 * j, 1024 * j + 1024))
 
-        def conv(k, h):
-            ts(B("pl%d" % (k % 2), h), R("q%d" % h, 0, 128), -OFF, Op.add)
+        def conv(k, j):
+            ts(B("pl%d" % (k % 2), j, 64), bank(k, j), -OFF, Op.add)
 
         def most(k, j):
             es, ed = ("EA", "EB")[k % 2], ("EB", "EA")[k % 2]
-            own = B("X", j % 2, 1024) if k == 0 else B("EC", j, 1024)
-            gat("v", B(ed, j, 1024), R(es), B("pl%d" % (k % 2), j, 64), own, Op.max)
-            dma(B("EC", j, 1024), B(ed, j, 1024), "s", "ec%d" % j)
+            if k == 0 and t == 0:
+                gat("v", B(ed, j, 1024), R(es, 0, L + 16), B("el", j, 64), B("X", j % 2, 1024), Op.max)
+            else:
+                own = B("X", j % 2, 1024) if k == 0 else B("EC", j, 1024)
+                gat("v", B(ed, j, 1024), R(es), B("pl%d" % (k % 2), j, 64), own, Op.max)
+            keep(k, j, ed)
 
-        def ended(j):
-            mm(R("q%d" % (2 + j % 2)), [(R("blkf"), B("PB", j, 512)), (R("blkf"), B("PB", 4 + j, 512))])
-            act(B("rg", j, 512), R("q%d" % (2 + j % 2)), AF.Copy)
+        def keep(k, j, src):
+            dma(B("EC", j, 1024), B(src, j, 1024), "s", "ec%d" % j)
 
         def fold1(j):
             mm(R("q%d" % (2 + j % 2)), [(ID(1.0), B("EA", j, 512)), (ID(-1.0), B("EA", 4 + j, 512))])
             act(B("ab", j, 512), R("q%d" % (2 + j % 2)), AF.Abs)
 
+        def fold0(j):
+            mm(R(FQ[j]), [(ID(1.0), B("X", j, 512))], True, False)
+
+        def ended(j):
+            mm(R(RQ[j]), [(R("blkf"), B("PB", j, 512)), (R("blkf"), B("PB", 4 + j, 512))], True, False)
+
         def fold2(j):
-            mm(R("q%d" % (4 + j % 2)), [(ID(1.0), B("rg", j, 512)), (ID(1.0), B("ab", j, 512))])
-            act(B("rr", j, 512), R("q%d" % (4 + j % 2)), AF.Relu)
+            mm(R(RQ[j]), [(ID(1.0), B("ab", j, 512))], False, True)
+            act(B("rr", j, 512), R(RQ[j]), AF.Relu)
 
         def fold3(j):
-            mm(R("q%d" % (7 * (j % 2))), [(ID(1.0), B("X", j, 512)), (ID(1.0), B("ab", j, 512)), (ID(-1.0), B("rr", j, 512))])
-            act(B("y32", j, 512), R("q%d" % (7 * (j % 2))), AF.Identity, M1, HALF)
+            mm(R(FQ[j]), [(ID(1.0), B("ab", j, 512)), (ID(-1.0), B("rr", j, 512))], False, True)
+            act(B("y32", j, 512), R(FQ[j]), AF.Identity, M1, HALF)
 
-        def fold4(h):
-            act(R(XW, A + 1024 * h, A + 1024 * h + 1024), B("y32", h, 1024), AF.Identity, -M1)
-            dma(B("X", h, 1024), R(XW, A + 1024 * h, A + 1024 * h + 1024), "g")
+        def fold4(j):
+            act(R(XW, A + 512 * j, A + 512 * j + 512), B("y32", j, 512), AF.Identity, -M1)
+            gcopy(B("X", j, 512), R(XW, A + 512 * j, A + 512 * j + 512))
 
-        def sums(h):
-            mm(B("q6", h, 64), wrap("SUMH", "EA", 1024 * h, 1024 * h + 1024) + wrap("SUMH", "EA", L + 1024 * h, L + 1024 * h + 1024), True, False)
-
-        def sums2(h):
-            mm(B("q6", h, 64), wrap("SUMH", "rr", 1024 * h, 1024 * h + 1024), False, True)
+        def sums(name, a, stop=False):
+            o = 144 * WN.index("SUMH")
+            mms([(R("q4", 128 + i, 256, 16), R(name, a + i, a + L, 16), R("wide", o + 15, o + 143, 16)) for i in range(16)], False, stop)
 
         def larger(j):
             gat("v", B("EB", j, 1024), R("EA"), B("sl", j, 64), B("EC", j, 1024), Op.max)
 
         def largersum(j):
-            mm(B("q%d" % (j // 2), j % 2, 64), wrap("SUM", "EB", 1024 * j, 1024 * j + 1024))
-        for k in range(K):
-            if k == 0:
-                laterlists(t)
-                for j in range(4):
-                    gat("a", B("PA", j, 1024), R("PS"), B("wl", j, 64))
-                    mm(R("q%d" % (j % 2), 0, 64), wrap("PTR", "PA", 1024 * j, 1024 * j + 1024))
-                    ts(B("pl0", j, 64), R("q%d" % (j % 2), 0, 64), -OFF, Op.add)
-                    if j:
-                        most(k, j - 1)
-                    if t == 0 and j == 0:
-                        mm(R("q4", 0, 384), [(ID(128.0), R("lc")), (ID(0.0625), R("hc"))])
-                        tt(R("d1"), R("cdi", 384, 512), R("d2"), Op.subtract)
-                        ts(R("wcl"), R("q4", 0, 384), -128 * OFF, Op.add)
-                        for i in range(3):
-                            tt(B("es", i), B("cf", i), B("nio", 0), Op.is_equal)
-                most(k, 3)
-                point(1, 0)
-                laterlists2()
-                conv(1, 0)
-                point(1, 1)
-            elif k < K - 1:
-                most(k, 0)
-                conv(k, 1)
-                point(k + 1, 0)
-                most(k, 1)
-                most(k, 2)
-                conv(k + 1, 0)
-                point(k + 1, 1)
-                if t == 0 and k < 8:
-                    widen(*(("SUM", 1.0), ("SUMH", -0.5), ("SUMK", 16384.0), ("SUMN", -8192.0), ("SWW", C(16)), ("R0", C(17)), ("R1", C(18)))[k - 1])
-                if k == 1:
-                    for s in range(2):
-                        for i in range(3):
-                            mm(B("q%d" % (2 + s), i), [(ID(1.0), B("hc", i)), (ID(1.0), B("lc", i)), (ID(-1.0), B("hb", s)), (ID(-1.0), B("lb", s))])
-                if k in (4, 6):
-                    act(B("eq", k // 5, 384), R("q%d" % (2 + k // 5), 0, 384), AF.Abs)
-                if k in (5, 7):
-                    act(B("ep", k // 6, 384), B("eq", k // 6, 384), AF.Relu, 1.0, -1.0)
-                if t == 0 and k == 8:
-                    act(R("kcol"), R("nio", 0, 16), AF.Identity, 0.5 - OFF)
-                    act(R("blkf"), R("blkm"), AF.Identity, 0.0, C(20))
-                    act(R("lz"), R("lc"), AF.Identity, -OFF)
-                most(k, 3)
-            else:
-                for j in range(4):
-                    for h in range(2):
-                        gat("v", B("EA", 4 * h + j, 512), R("EB"), B("pl1", 4 * h + j, 32), B("EC", 4 * h + j, 512), Op.max)
-                        if j % 2:
-                            i = 2 * h + j // 2
-                            dma(B("EC", i, 1024), B("EA", i, 1024), "s", "ec%d" % i)
-                        if j == 0 and h == 0:
-                            conv(k, 1)
-                            for i in range(4):
-                                ended(i)
-                    fold1(j)
-                    if j > 0:
-                        fold2(j - 1)
-                    if j > 1:
-                        fold3(j - 2)
-                    if j == 1:
-                        sums(0)
-                    if j == 2:
-                        sums2(0)
-        for j in (0, 2, 1, 3):
-            larger(j)
-        fold2(3)
-        fold3(2)
-        sums(1)
-        fold4(0)
-        sums2(1)
-        fold3(3)
-        act(R("s01"), R("q6", 0, 128))
-        fold4(1)
-        largersum(0)
-        largersum(2)
-        largersum(1)
-        largersum(3)
-        mm(R("q7", 0, 128), wrap("SUM", XW, A, A + L))
-        for h in range(2):
-            tt(B("bf", h), R("q%d" % h, 0, 128), R("s01"), Op.add)
-        hi64(R("hb"), R("bf"))
-        unwrap(HI, R("hb"))
-        tt(R("lb"), R("bf"), R("hb"), Op.subtract)
-        unwrap(LO, R("lb"))
-        hi64(R("hs"), R("q7", 0, 128))
-        tt(R("ls"), R("q7", 0, 128), R("hs"), Op.subtract)
+            mm(B(LQ[j % 2], j // 2, 64), [(R("s01"), B("idf", j % 2, 64))] + wrap("SUM", "EB", 1024 * j, 1024 * j + 1024))
 
-        def back(j):
-            gat("a", B("PA", j, 1024), R("PS", 0, 4096), B("bl", j, 64))
-            mm(B("q%d" % (j // 2), j % 2, 64),
-               [(ID(1.0), B("hb", j, 64)), (ID(1.0), B("lb", j, 64)), (ID(16384.0), B("fr", j, 64))]
+        def linksum(h):
+            cp(B("bh", h), R(LQ[h], 0, 128))
+            unwrap("PT", HI, B("bh", h), L * h)
+            tt(B("bo", h), R(LQ[h], 0, 128), B("bh", h), Op.subtract)
+            unwrap("PT", LO, B("bo", h), L * h)
+
+        def turn(k):
+            return (0, 1, 2, 3) if k < K - 3 else (0, 2, 1, 3)
+
+        def side(k, j):
+            if t:
+                if (k, j) == (1, 1):
+                    act(R("lk", 0, 512), R("q5"))
+                if (k, j) == (2, 1):
+                    act(cc, R("q7", 0, 256))
+            if k == K - 2 and j < 2:
+                fold0(j)
+            if (k, j) == (4, 1):
+                laterlists("q6")
+            if (k, j) == (5, 1):
+                laterlists2("q6")
+        if t == 0:
+            ts(R("wl"), R("q6", 0, 256), -256 * OFF, Op.add)
+            most(0, 0)
+            first("a", 0)
+            first("v", 3)
+            first("a", 1)
+            first("v", 2)
+            conv(0, 0)
+            twice2(1, 4)
+            most(0, 1)
+            point(1, 0)
+            conv(0, 1)
+            conv(0, 2)
+            conv(0, 3)
+            point(1, 1)
+            most(0, 2)
+            conv(1, 0)
+            point(1, 2)
+            most(0, 3)
+            ts(R("thf"), R("thi"), 0.5, Op.mult)
+        else:
+            first("v", 3)
+            first("a", 0)
+            conv(0, 3)
+            first("a", 1)
+            most(0, 3)
+            conv(0, 0)
+            first("a", 2)
+            most(0, 0)
+            conv(0, 1)
+            point(1, 0)
+            point(1, 1)
+            most(0, 1)
+            conv(0, 2)
+            conv(1, 0)
+            point(1, 2)
+            most(0, 2)
+        conv(1, 1)
+        point(1, 3)
+        for k in range(1, K - 1):
+            for j in range(4):
+                most(k, turn(k)[j])
+                conv(k + j // 2, turn(k + j // 2)[(j + 2) % 4])
+                point(k + 1, turn(k + 1)[j])
+                side(k, j)
+        k = K - 1
+        for j in range(4):
+            for h in range(2):
+                gat("v", B("EA", 4 * h + j, 512), R("EB"), B("pl1", 4 * h + j, 32), B("EC", 4 * h + j, 512), Op.max)
+                if j == 0:
+                    conv(k, 1 + 2 * h)
+                if j % 2:
+                    i = 2 * h + j // 2
+                    keep(k, i, "EA")
+            fold1(j)
+            ended(j)
+            fold2(j)
+        mm(R("q4", 128, 256), [(R("zer"), R("zer"))], True, False)
+        sums("EA", 0)
+        sums("EA", L)
+        sums("rr", 0, True)
+        act(R("s01"), R("q4", 128, 256))
+        fold0(2)
+        fold0(3)
+        for j in range(4):
+            fold3(j)
+        for j in range(4):
+            fold4(j)
+        larger(0)
+        largersum(0)
+        larger(2)
+        largersum(2)
+        larger(1)
+        largersum(1)
+        larger(3)
+        linksum(0)
+        largersum(3)
+        linksum(1)
+        if not last:
+            weave(weights("PTR", (JH, JL, CH, CL, CC)))
+
+        def back(e, j):
+            gat(e, B("PA", j, 1024), R("PT", 0, 2 * L), B("bl", j, 64))
+            o = 2 * (j % 2) + j // 2
+            mm(B("q2", j, 64),
+               [(ID(1.0), B("bh", o, 64)), (ID(1.0), B("bo", o, 64)), (ID(16384.0), B("fr", j, 64))]
                + ([(ID(-16384.0), B("jb", j, 64))] if t else []) + wrap("TWO", "PA", 1024 * j, 1024 * j + 1024))
 
-        def nearsum(i):
-            mm(R("q%d" % (3 + i), 0, 128),
-               [(ID(1.0), B("cst", 0)), (ID(2.0 ** 26), B("es", i)), (ID(-8192.0), R("hs")), (ID(-8192.0), R("ls"))]
-               + wrap("SUMK", "MC", i * L, i * L + L), True, False)
-        for j in range(6):
-            gat("v", B("MC", j, 1024), R(XW, A, A + L + 16), B("cl", j, 64), B("X", j % 2, 1024), Op.max)
-        nearsum(0)
-        back(0)
-        back(1)
-        nearsum(1)
-        back(2)
-        back(3)
-        for h in range(2):
-            ts(B("fr", h), R("q%d" % h, 0, 128), R("thf", t, t + 1), Op.is_ge)
+        def mc(i, h, a=0, b=1024):
+            o = 1024 * h
+            gat("v", R("MC", i * L + o + a, i * L + o + b), XF, R("cl", (i * L + o + a) // 16, (i * L + o + b) // 16), R("X", o + a, o + b), Op.max)
+
+        def mcsum(i, h):
+            if h == 0:
+                mm(R("q%d" % (3 + i), 0, 128),
+                   [(ID(1.0), B("cst", 0)), (ID(2.0 ** 26), B("es", i)), (ID(-8192.0), R("hs")), (ID(-8192.0), R("ls"))], True, False)
+            mm(B("q%d" % (3 + i), h, 64), wrap("SUMK", "MC", i * L + 1024 * h, i * L + 1024 * h + 1024), False, False)
+        mm(R("q7", 0, 128), wrap("SUM", XW, A, A + L))
+        act(R("hs"), R("q7", 0, 128))
+        mc(0, 0)
+        back("a", 0)
+        back("v", 2)
+        back("a", 1)
+        back("a", 3)
+        if t == 0:
+            mm(R("q6", 0, 384), [(ID(128.0), R("lc")), (ID(0.0625), R("hc"))])
+        for s in range(2):
+            near(s)
+            near2(s)
+            near3(s)
+        tt(R("ls"), R("q7", 0, 128), R("hs"), Op.subtract)
+        unwrap("PT", HI, R("hs"), SC0)
+        unwrap("PT", LO, R("ls"), SC0)
+        mc(2, 0)
+        mc(1, 0)
+        if t == 0:
+            ts(R("wcl"), R("q6", 0, 384), -129 - 128 * OFF, Op.add)
+        ts(R("fr"), R("q2", 0, 256), R("thf", t, t + 1), Op.is_ge)
         tt(R("fb"), B("fr", 0), B("fr", 1), Op.max)
-        unwrap(CAME, R("fb"))
-        unwrap(HI, R("hs"))
-        unwrap(LO, R("ls"))
-        unwrap(LOW, B("fr", 0), L)
+        unwrap("PT", FRE, R("fb"), SC0)
+        unwrap("PT", LOW, B("fr", 0), TO0)
+        if not last:
+            unwrap("PS", OPEN, R("fr"))
         mm(R("q2", 0, 128), [(R("blkm"), R("fb"))])
         mm(R("q7", 0, 128), [(R("utm"), R("fb"))])
-        for s in range(2):
-            for i in range(3):
-                mm(B("q%d" % s, i), [(ID(1.0), B("ep", 3 * s + i)), (ID(-1.0), B("fr", s))])
-        nearsum(2)
+        tt(R("sw"), R("q2", 0, 128), R("upto"), Op.mult)
         run("v", [R("one"), R("q2", 0, 128)], [R("cum")],
-            lambda: g.vector.tensor_tensor_scan(T.cum[:], T.one[:], T.q2[:, 0:128], 0.0, Op.mult, Op.add))
-        for q in range(NV, 16):
-            act(B("sg", q), R("cum"), AF.Sign, R("kcol", q, q + 1), -1.0, R("acc", q, q + 1))
-        tt(R("pw", 0, 128), R("cum"), R("q7", 0, 128), Op.subtract)
-        for q in range(NV):
-            ts(B("sw", q), R("cum"), R("kcol", q, q + 1), Op.is_le)
-        for q in range(NV):
-            total(R("acc", q, q + 1), B("sw", q))
-        cp(R("l1", 0, NV), R("acc", 0, NV))
-        cp(R("colb", 0, NV), R("acc", 0, NV))
-        act(R("colb", NV, 16), R("acc", NV, 16), AF.Identity, 64.0, 0.5)
+            lambda: g.vector.tensor_tensor_scan(T.cum[:], T.one[:], T.q2[:, 0:128], 0.0, Op.mult, Op.add), us(128))
+        total(C(8), R("sw"))
+        act(R("cumb"), R("cum"))
+        ts(B("cmp", 0, 256), R("rkb"), C(8), Op.is_ge)
+        mm(R("q2", 128, 144), wrap("SUM", "cmp", 0, 256))
+        tt(R("pw", 0, 128), R("q7", 0, 128), R("cum"), Op.add)
+        mm(R("q6", 0, 16), [(l, R("cumb", i, 128, 8)) for i, (l, r) in enumerate(wrap("ROW0", "cmp", 0, 256)[:8])])
+        act(R("tab", 0, 16), R("q6", 0, 16), AF.Identity, C(7))
+        cp(R("l1", 0, 16), R("q2", 128, 144))
+        cp(R("colb", 0, 16), R("q2", 128, 144))
+        gat("v", B("cmp", 1, 256), R("tab"), R("l1", 0, 16), R("rk"), Op.is_le)
+        mm(R("q6", 16, 32), [(ID(8.0), R("colb", 0, 16))] + wrap("SUM", "cmp", 256, 512))
+        cp(R("l1", 16, 32), R("q6", 16, 32))
+        cp(R("colb", 16, 32), R("q6", 16, 32))
+        gat("v", B("cmp", 2, 256), R("pw"), R("l1", 16, 32), R("rk"), Op.is_le)
+        mm(R("q7", 128, 144), [(ID(16.0), R("colb", 16, 32))] + wrap("SUM", "cmp", 512, 768))
+        cp(R("l2"), R("q7", 128, 144))
+        gat("v", R("blk%d" % t), XF, R("l2"))
+        send(t)
         for s in range(2):
+            mms([(R("q%d" % s, 0, 384), ID(1.0), B("ep", s, 384))] + [(B("q%d" % s, i), ID(-1.0), B("fr", s)) for i in range(3)])
             act(B("eq", s, 384), R("q%d" % s, 0, 384), AF.Relu)
-        ts(R("l1", NV, 16), R("acc", NV, 16), 0.5, Op.mult, 64.0, Op.add)
-        gat("v", R("cmp"), R("pw"), R("l1"), R("rk"), Op.is_le)
-        mm(R("q2", 0, 16), [(ID(16.0), R("colb"))] + wrap("SUM", "cmp", 0, 256))
-        ts(R("t1"), R("fr"), FREE + OFF, Op.mult)
-        cp(R("l2"), R("q2", 0, 16))
-        gat("v", R("blk%d" % t), R(XW, A, A + L + 16), R("l2"))
-        order("g", [R("blk%d" % t)], [])
-        rid, pid, _ = topo.addr(nxt)
-        ne = len(topo.engines(core, nxt))
-        g.remote_dma(T[XW][:, 0:A], T["blk%d" % t][:], T.sem["arr%d" % t], T.sem.sent, pid, rid, topo.mask(core, nxt))
-        cnt["sent"] = cnt.get("sent", 0) + ne
-        cnt["arr%d" % t] = ne
-        hist.setdefault(XW, []).append((0, A, None, True, ("arr%d" % t, ne), "r"))
-        gat("a", B("SC", 0, L), R("PS", 0, L), B("wcl", 0))
-        gat("v", B("SC", 1, L), R("PS", 0, L), B("wcl", 1))
-        gat("v", R("SC", 2 * L, 2 * L + 512), R("PS", 0, L), R("wcl", 256, 288))
-        gat("a", R("SC", 2 * L + 512, 3 * L), R("PS", 0, L), R("wcl", 288, 384))
-        if not last:
-            unwrap(OPEN, R("fr"))
-        for i in range(3):
-            mm(R("q%d" % (3 + i), 0, 128), [(ID(2.0 ** 26), B("eq", i)), (ID(2.0 ** 26), B("eq", 3 + i))] + wrap("SWW", "SC", i * L, i * L + L)
-               + ([(ID(1.0), B("cst", i))] if i else []) + [(ID(1.0), B("hc", i)), (ID(1.0), B("lz", i))], False, True)
-        for h in range(2):
+
+        def sc(e, i, h):
+            gat(e, B("SC", 2 * i + h, 1024), R("PT", SC0, SC0 + L), B("wcl", 2 * i + h, 64))
+            mm(B("q%d" % (3 + i), h, 64), wrap("SWW", "SC", i * L + 1024 * h, i * L + 1024 * h + 1024), False, False)
+
+        def key(i):
+            mm(R("q%d" % (3 + i), 0, 128), [(ID(2.0 ** 26), B("eq", i)), (ID(2.0 ** 26), B("eq", 3 + i))]
+               + ([(ID(i - 1.0), B("cst", 1))] if i != 1 else []) + [(ID(1.0), B("hc", i)), (ID(1.0), B("lz", i))], False, True)
+
+        def arrival(h):
             a, b = 3 * L + 1024 * h, 3 * L + 1024 * h + 1024
             gat("v", R("MC", a, b), R(XW, 0, A), B("cl", 6 + h, 64), B("X", h, 1024), Op.max)
+            mm(B("q6", h, 64), wrap("SUMK", "MC", a, b), False, False)
+
+        def arrived(h):
+            a, b = 3 * L + 1024 * h, 3 * L + 1024 * h + 1024
             gat("a", R("SC", a, b), R(XW, 0, A), B("cl", 6 + h, 64))
-            mm(B("q6", h, 64),
-               [(ID(1.0), R("cst", 384, 448)), (ID(-2.0 ** 28), B("fb", h, 64)), (ID(-8192.0), B("hs", h, 64)), (ID(-8192.0), B("ls", h, 64))]
-               + wrap("SUMN", "SC", a, b) + wrap("SUMK", "MC", a, b) + [(ID(1.0), R("cst", 512, 576))])
-        if not last:
-            mm(R("q1", 0, 256), [(ID(1.0), R("c")), (ID(1.0), R("fr"))])
-            act(R("c"), R("q1", 0, 256), AF.Sign)
-            unwrap(CAME, R("c"))
-        cp(R("km"), R("q3", 0, 128))
-        tt(R("km"), R("km"), R("q4", 0, 128), Op.min)
-        tt(R("ki"), R("km"), R("q5", 0, 128), Op.min)
-        ts(R("ti"), R("ki"), 2047, Op.bitwise_and)
-        tt(R("mix"), R("q6", 0, 128), R("ki"), Op.is_lt)
-        unwrap(MIX, R("mix"), L)
-        ts(R("tq"), R("ti"), OFF, Op.add)
-        hi16(R("hw"), R("tq"))
-        unwrap(HI, R("hw"), L)
-        tt(R("lw"), R("tq"), R("hw"), Op.subtract)
-        unwrap(LO, R("lw"), L)
-        mm(R("q7", 0, 128), [(ID(1.0), B("r16", 0)), (ID(-8192.0), B("fr", 0)), (ID(8192.0), R("mix"))])
-        mm(R("q7", 128, 256), [(ID(1.0), B("r16", 0)), (ID(-8192.0), B("fr", 1)), (ID(8192.0), B("fr", 0)), (ID(8192.0), R("mix"))])
-        mm(R("q2", 0, 128), [(ID(128.0), R("lw")), (ID(0.0625), R("hw"))])
-        act(R("wa"), R("q7", 0, 256), AF.Identity, C(19))
-        tt(R("ml32"), R("d1"), R("mix"), Op.mult)
-        ts(R("tl"), R("q2", 0, 128), -128 * OFF, Op.add)
-        tt(R("ml32"), R("ml32"), R("d2"), Op.add)
-        ts(R("to"), R("ti"), -float(FREE), Op.add)
-        cp(R("ml"), R("ml32"))
+            mm(B("q6", h, 64), wrap("SUMN", "SC", a, b), False, h == 1)
+        YQ = ("q0", "q1", "q2", "q7")
 
         def mixing(j):
-            mm(R("q%d" % (2 + j)), [(ID(0.5), R("mh")), (ID(0.5), B("X", j, 512)), (ID(0.5), B("ab", j, 512))])
+            mm(R(YQ[j]), [(ID(0.5), R("mh")), (ID(0.5), B("X", j, 512))], True, False)
 
-        def rounding(j):
-            ts(B("X", j, 512), R("q%d" % (2 + j)), M1, Op.add, M1, Op.subtract)
+        def mixing2(j):
+            mm(R(YQ[j]), [(ID(0.5), R("SC", 3 * L + 512 * j, 3 * L + 512 * j + 512))], False, True)
 
-        def blend(h):
-            gat("a", B("ab", h, 1024), R(XW, 0, A + L), B("ml", h, 64))
+        def mixing3(j):
+            ts(R(XW, A + YO + 512 * j, A + YO + 512 * j + 512), R(YQ[j]), M1, Op.add, M1, Op.subtract)
+        for i in range(3):
+            mcsum(i, 0)
+        mm(R("q6", 0, 128), [(ID(1.0), B("cst", 2)), (ID(-2.0 ** 28), R("fb")), (ID(1.0), B("cst", 3)), (ID(-8192.0), R("hs")), (ID(-8192.0), R("ls"))], True, False)
+        for j in range(4):
+            mixing(j)
+        sc("a", 0, 0)
+        for a in (0, 256, 512, 768):
+            mc(0, 1, a, a + 256)
+        mcsum(0, 1)
+        sc("a", 0, 1)
+        key(0)
+        for a in (0, 256, 512):
+            mc(1, 1, a, a + max(a, 256))
+        mcsum(1, 1)
+        sc("a", 1, 0)
+        sc("a", 1, 1)
+        key(1)
+        mc(2, 1)
+        mcsum(2, 1)
+        sc("a", 2, 0)
+        sc("v", 2, 1)
+        key(2)
+        cp(R("km"), R("q3", 0, 128))
+        arrival(0)
+        arrived(0)
+        mixing2(0)
+        mixing2(1)
+        tt(R("km"), R("km"), R("q4", 0, 128), Op.min)
+        arrival(1)
+        arrived(1)
+        tt(R("ki"), R("km"), R("q5", 0, 128), Op.min)
+        ts(R("ti"), R("ki"), 2047, Op.bitwise_and)
+        ts(R("tq"), R("ti"), OFF, Op.add)
+        hi16(R("hw"), R("tq"))
+        unwrap("PT", HI, R("hw"), TO0)
+        tt(R("mix"), R("q6", 0, 128), R("ki"), Op.is_lt)
+        unwrap("PT", MIX, R("mix"), TO0)
+        tt(R("lw"), R("tq"), R("hw"), Op.subtract)
+        unwrap("PT", LO, R("lw"), TO0)
 
-        def joined():
+        def blend(e, h):
+            gat(e, B("X", h, 1024), R(XW, A, A + YO + L), B("ml", h, 64))
+
+        def mutual(e, h):
+            gat(e, B("PA", h, 1024), R("PT", TO0, TO0 + L), B("tl", h, 64))
+        mm(R("q6", 128, 256), [(ID(128.0), R("lw")), (ID(0.0625), R("hw"))])
+        mm(R("q6", 256, 384), [(ID(1.0), B("r16", 0)), (ID(float(YO)), R("mix"))])
+        mixing2(2)
+        mixing2(3)
+        mm(R("q5", 256, 384), [(ID(1.0), B("r16", 0)), (ID(-8192.0), B("fr", 0))])
+        mm(R("q5", 384, 512), [(ID(1.0), B("r16", 0)), (ID(-8192.0), B("fr", 1)), (ID(8192.0), B("fr", 0))])
+        act(R("wa"), R("q5", 256, 512), AF.Identity, C(4))
+        if last:
+            mm(R("q3", 0, 256), [(ID(1.0), hb), (ID(1.0), lb), (ID(4096.0), R("fr"))])
+        else:
+            mm(R("q3", 0, 256), [(ID(2048.0), R("fr")), (ID(-1.0), hb)])
+            mm(R("q3", 256, 512), [(ID(31.25), R("fr")), (ID(-1.0), lb)])
+            mm(R("q4", 0, 256), [(ID(1.0), R("fr")), (ID(-1.0), cc)])
+            act(R("ct", 0, 512), R("q3"), AF.Relu)
+            act(R("ct", 512, 768), R("q4", 0, 256), AF.Relu)
+        mixing3(0)
+        mixing3(1)
+        ts(R("tl"), R("q6", 128, 256), -128 * OFF, Op.add)
+        ts(R("ml"), R("q6", 256, 384), C(1), Op.add)
+        mixing3(2)
+        mixing3(3)
+        if last:
+            for h in range(2):
+                mm(B("q4", h), [(ID(1.0), R("hw")), (ID(1.0), R("lw")), (ID(-1.0), B("cst", 1)), (ID(-16.25), R("oneb"))])
+            ts(R("q3", 256, 512), R("q3", 0, 256), -OFF, Op.add, 2048.0, Op.min)
+        else:
+            for i, row in enumerate((CH, CL, CC)):
+                dma(R("PS", 0, 4096, row=row), B("ct", i, 256), after=R("tl"))
+            for h in range(2):
+                mm(B("q4", 2 + h), [(ID(-1.0), R("lw")), (ID(31.25), R("oneb"))])
+            mm(R("q1", 0, 128), [(ID(-1.0), R("hw")), (ID(4096.0), R("oneb"))], True, False)
+        mm(R("q0", 0, 128), [(ID(-8192.0), R("mix"))], True, False)
+        mutual("v", 0)
+        mutual("a", 1)
+        for h in range(2):
+            mm(B("q0", h, 64), wrap("R0", "PA", 1024 * h, 1024 * h + 1024), False, h == 1)
+        if last:
+            blend("a", 0)
+            dma(T.yx[:, 0:1024], B("X", 0, 1024))
+            blend("a", 1)
             for h in range(2):
                 tt(B("jb", h), R("q0", 0, 128), B("wa", h), Op.is_equal)
-            if not last:
-                unwrap(JOIN, R("jb"))
-            for h in range(2):
-                tt(B("jj", h), B("jb", h), R("to"), Op.mult)
-            tt(R("m"), R("m"), R("jj"), Op.add)
-        if last:
-            blend(0)
-            mixing(0)
-            mixing(1)
-        gat("v", B("PA", 0, 1024), R("PS", L, 2 * L), B("tl", 0, 64))
-        gat("a", B("PA", 1, 1024), R("PS", L, 2 * L), B("tl", 1, 64))
-        mm(R("q0", 0, 128), wrap("R0", "PA", 0, L))
-        tt(R("m"), R("m"), R("t1"), Op.max)
-        if last:
-            blend(1)
-            mixing(2)
-            mixing(3)
-            rounding(0)
-            rounding(1)
-            dma(T.yx[:, 0:1024], B("X", 0, 1024))
-            joined()
-            ts(R("yo"), R("m"), -OFF, Op.add, 2048.0, Op.min)
+            tt(R("jj"), R("q4", 0, 256), R("jb"), Op.mult)
+            tt(R("yo"), R("q3", 256, 512), R("jj"), Op.add)
+            dma(T.yx[:, 1024:L], B("X", 1, 1024))
             dma(T.yn[:], R("yo"))
-            rounding(2)
-            rounding(3)
-            dma(T.yx[:, 1024:L], B("X", 1, 1024), "a")
         else:
-            mm(R("q1", 0, 128), wrap("R1", "PA", 0, L))
-            blend(0)
-            blend(1)
-            joined()
-            hi16(R("hb"), R("m"))
-            unwrap(HI, R("hb"))
+            jh, jl, e0 = B("jn", 0, 256), B("jn", 1, 256), B("jn", 2, 256)
+            ch, cl, ca = B("ct", 0, 256), B("ct", 1, 256), B("ct", 2, 256)
             for h in range(2):
-                tt(B("e0", h), R("q1", 0, 128), B("wa", h), Op.is_equal)
-            unwrap(LESS, R("e0"))
-            tt(R("lb"), R("m"), R("hb"), Op.subtract)
-            unwrap(LO, R("lb"))
-            mixing(0)
-            mixing(1)
-            steplist(1)
-            mixing(2)
-            mixing(3)
-            for j in range(4):
-                rounding(j)
-            cp(R("EA", 0, L), R("X"))
-            cp(R("EA", L, 2 * L), R("X"))
+                mm(B("q1", h, 64), wrap("R1", "PA", 1024 * h, 1024 * h + 1024), False, h == 1)
+            mm(R("q6", 0, 256), [(ID(256.0), lb), (ID(256.0), cl), (ID(0.0625), hb), (ID(0.0625), ch), (ID(128.0), cc), (ID(128.0), ca)], True, False)
+            blend("a", 0)
+            blend("a", 1)
+            for h in range(2):
+                tt(B("jb", h), R("q0", 0, 128), B("wa", h), Op.is_equal)
+            unwrap("PS", JOIN, R("jb"))
+            tt(jl, R("q4", 256, 512), R("jb"), Op.mult)
+            unwrap("PS", JL, jl)
+            for h in range(2):
+                tt(H(jh, h), R("q1", 0, 128), B("jb", h), Op.mult)
+            unwrap("PS", JH, jh)
+            gcopy(B("EA", 0, 1024), B("X", 0, 1024))
+            gcopy(B("EA", 2, 1024), B("X", 0, 1024))
+            mm(R("q6", 0, 256), [(ID(-256.0), jl), (ID(-0.0625), jh)], False, True)
+            ts(e0, jh, 2048.0, Op.is_gt)
+            ts(R("wl"), R("q6", 0, 256), -256 * OFF, Op.add)
+            cp(B("EA", 1, 1024), B("X", 1, 1024))
+            cp(B("EA", 3, 1024), B("X", 1, 1024))
+            for i in range(3):
+                mm(R(("q5", "q5", "q7")[i], 256 * (i % 2), 256 * (i % 2) + 256),
+                   [(ID(1.0), B("lk", i, 256)), (ID(1.0), B("ct", i, 256)), (ID(-1.0), B("jn", i, 256))] + ([] if i else [(ID(2048.0), e0)]))
+    schedule()
     for s, n in cnt.items():
         if n:
             wait("g", (s, n))

from concourse.mybir import AluOpType as Op, AxisListType as AX, ActivationFunctionType as AF

L = 2048
A = 256
RO = 2
K = 10
FREE = 2063
END = FREE + L
OFF = 16.25
C16A, C16B = 2.0 ** 27 - 8, 2.0 ** 27 + 16
M1 = 12582912.0
HALF = 0.5 - 2.0 ** -11
YO = L + 16
BF, F, I, U = "bfloat16", "float32", "int32", "uint16"
HI, LO, CAME, OPEN, JOIN, JH, JL, CH, CL, CC = range(10)
W0 = 12
FRE, LOW, MIX = 2, 3, 4
SC0, TO0 = 2 * L, 3 * L
ROWS = {"WTWO": {W0: 1.0, W0 + 1: 1.0},
        "PTR": {HI: 1.0, LO: 1.0, CAME: 2048.0, JH: -1.0, JL: -1.0, CH: 1.0, CL: 1.0, CC: 2048.0},
        "TWO": {HI: 1.0, LO: 1.0}, "SWW": {HI: -8192.0, LO: -8192.0, FRE: -2.0 ** 26},
        "R0": {HI: 1.0, LO: 1.0, MIX: 4096.0}, "R1": {LOW: -2048.0}, "ROW0": {0: 1.0}}
EVEN = {"FOUR": (W0, 1.0), "SUM": (0, 1.0), "SUMH": (0, -0.5), "SUMK": (0, 16384.0), "SUMN": (0, -8192.0)}
WN = list(ROWS) + list(EVEN)
IDS = [128.0, 0.0625, 1920.0, -1.0, 1.0, 15.0, 256.0, -64.0, 992.0, 2048.0, 16384.0, -16384.0, 2.0 ** 26, -8192.0,
       8192.0, -2.0 ** 28, 16.0, 0.5, 31.25, -16.25, 4096.0, float(YO), -256.0, -0.0625, 8.0]
CST = [3 * 2.0 ** 24, 2048.0, 15 * 2.0 ** 24, 6144.0]

SCRATCH = {
    "nbi": ("sbuf", [128, 256], I), "cdi": ("sbuf", [128, 512], I), "thi": ("sbuf", [128, 2], I),
    "thf": ("sbuf", [128, 2], F),
    "X": ("sbuf", [128, L], BF), "EA": ("sbuf", [128, 4112], BF), "EB": ("sbuf", [128, 4112], BF),
    "EC": ("sbuf", [128, 4096], BF),
    "PA": ("sbuf", [128, 4112], BF), "PB": ("sbuf", [128, 4112], BF), "PS": ("sbuf", [128, 4112], BF),
    "PT": ("sbuf", [128, 4 * L], BF),
    "XW0": ("sbuf", [128, A + YO + L], BF), "XW1": ("sbuf", [128, A + YO + L], BF),
    "blk0": ("sbuf", [128, A], BF), "blk1": ("sbuf", [128, A], BF),
    "ab": ("sbuf", [128, L], BF), "rr": ("sbuf", [128, L], BF), "y32": ("sbuf", [128, L], F),
    "MC": ("sbuf", [128, 4 * L], BF), "SC": ("sbuf", [128, 4 * L], BF),
    "wide": ("sbuf", [128, 144 * len(WN)], BF), "idm": ("sbuf", [128, 128 * len(IDS)], BF), "idf": ("sbuf", [128, 128], F),
    "blkm": ("sbuf", [128, 128], BF), "utm": ("sbuf", [128, 128], BF), "zer": ("sbuf", [128, 128], BF),
    "blkf": ("sbuf", [128, 128], BF), "oneb": ("sbuf", [128, 128], BF),
    "cst": ("sbuf", [128, 128 * len(CST)], BF), "mh": ("sbuf", [128, 512], BF),
    "pi": ("sbuf", [128, 4], I), "col": ("sbuf", [128, 16], F), "ew": ("sbuf", [128, 16], F),
    "rk": ("sbuf", [128, 256], F), "r16": ("sbuf", [128, 256], BF),
    "nio": ("sbuf", [128, 256], F), "kcol": ("sbuf", [128, 16], F),
    "lk": ("sbuf", [128, 768], BF), "ct": ("sbuf", [128, 768], BF), "jn": ("sbuf", [128, 768], BF),
    "fr": ("sbuf", [128, 256], BF), "jb": ("sbuf", [128, 256], BF), "sq": ("sbuf", [128, 256], BF),
    "l0": ("sbuf", [128, 256], BF), "bh": ("sbuf", [128, 256], BF), "bo": ("sbuf", [128, 256], BF),
    "hs": ("sbuf", [128, 128], BF), "ls": ("sbuf", [128, 128], BF),
    "hw": ("sbuf", [128, 128], BF), "lw": ("sbuf", [128, 128], BF),
    "t1": ("sbuf", [128, 256], F), "t2": ("sbuf", [128, 256], F), "nn": ("sbuf", [128, 256], F),
    "s01": ("sbuf", [128, 128], F),
    "wl": ("sbuf", [128, 256], U), "el": ("sbuf", [128, 256], U), "sl": ("sbuf", [128, 256], U), "bl": ("sbuf", [128, 256], U),
    "pl0": ("sbuf", [128, 256], U), "pl1": ("sbuf", [128, 256], U),
    "cl": ("sbuf", [128, 512], U), "wcl": ("sbuf", [128, 384], U), "cf": ("sbuf", [128, 384], F),
    "hc": ("sbuf", [128, 384], BF), "lc": ("sbuf", [128, 384], BF), "lz": ("sbuf", [128, 384], BF),
    "es": ("sbuf", [128, 384], BF), "eq": ("sbuf", [128, 768], BF), "ep": ("sbuf", [128, 768], BF),
    "sw": ("sbuf", [128, 128], F), "upto": ("sbuf", [128, 128], F), "cumb": ("sbuf", [128, 128], BF),
    "fb": ("sbuf", [128, 128], BF), "cum": ("sbuf", [128, 128], F), "pw": ("sbuf", [128, 144], F),
    "one": ("sbuf", [128, 128], F), "tab": ("sbuf", [128, 32], F), "rkb": ("sbuf", [128, 256], BF),
    "colb": ("sbuf", [128, 32], BF), "l1": ("sbuf", [128, 32], U), "l2": ("sbuf", [128, 16], U),
    "cmp": ("sbuf", [128, 768], BF),
    "km": ("sbuf", [128, 128], F), "ki": ("sbuf", [128, 128], I), "ti": ("sbuf", [128, 128], I),
    "tq": ("sbuf", [128, 128], F), "tl": ("sbuf", [128, 128], U),
    "ml": ("sbuf", [128, 128], U), "mix": ("sbuf", [128, 128], BF),
    "wa": ("sbuf", [128, 256], F), "jj": ("sbuf", [128, 256], F), "yo": ("sbuf", [128, 256], F),
}
for _b in range(8):
    SCRATCH["q%d" % _b] = ("psum", [128, 512], F)
LOOSE, SLACK, MARGIN, WAKE, GATHER = {"p": 30, "s": 12, "a": 30, "v": 30, "g": 1}, 0.1, 0.4, 0.1, 1.5
NDMA = 72
SEMAPHORES = (["sv", "sa", "sp", "sg", "sent"] + ["arr%d" % t for t in range(RO)] + ["ec%d" % i for i in range(4)]
              + ["dm%d" % i for i in range(NDMA)])


def rank_program(g, core, T, topo):
    rank = T.rank_of(core)
    if rank is None:
        return
    nxt = T.cores[(rank + 1) % len(T.cores)]
    Q = {"v": g.vector, "a": g.scalar, "p": g.tensor, "s": g.sync, "g": g}
    cnt = {"sv": 0, "sa": 0, "sp": 0, "sg": 0}
    known = {e: {} for e in Q}
    clock = {}
    hist = {}
    ndma = [0]
    todo, done = [], {}

    def R(name, a=0, b=None, step=1, row=None):
        t = T[name]
        if b is None:
            b = t.shape[1]
        cs = slice(a, b) if step == 1 else slice(a, b, step)
        return (t[:, cs] if row is None else t[row::16, cs], name, a, b, row, len(range(a, b, step)))

    def B(name, i, n=128):
        return R(name, n * i, n * i + n)

    def wait(e, tok):
        s, n = tok
        if known[e].get(s, 0) >= n:
            return
        Q[e].wait_ge(T.sem[s], n)
        known[e][s] = n
        for s2, n2 in clock.get(tok, {}).items():
            if known[e].get(s2, 0) < n2:
                known[e][s2] = n2

    def order(e, reads, writes, cont=False):
        need = {}
        for lst, w in ((reads, False), (writes, True)):
            for r in lst:
                ps = r[1][0] == "q"
                for a, b, row, w2, tok, e2 in hist.get(r[1], []):
                    apart = b <= r[2] or r[3] <= a
                    if ps:
                        if e2 == e and (cont or apart or not (w or w2)):
                            continue
                    elif not (w or w2) or apart or (row is not None and r[4] is not None and row != r[4]):
                        continue
                    need[tok[0]] = max(need.get(tok[0], 0), tok[1])
        for s, n in need.items():
            if not any(clock.get(tok, {}).get(s, 0) >= n for tok in need.items()):
                wait(e, (s, n))

    def note(e, tok, reads, writes):
        clock[tok] = dict(known[e])
        for lst, w in ((reads, False), (writes, True)):
            for r in lst:
                h = hist.setdefault(r[1], [])
                if r[1][0] == "q":
                    h[:] = [x for x in h if x[5] == e and not (w and r[2] <= x[0] and x[1] <= r[3])]
                elif w:
                    h[:] = [x for x in h if not (r[2] <= x[0] and x[1] <= r[3] and (r[4] is None or r[4] == x[2]))]
                h.append((r[2], r[3], r[4], w, tok, e))

    def issue(e, reads, writes, call, cont, kind):
        order(e, reads, writes, cont)
        if kind == "remote":
            return call()
        s, n = "s" + e, 1
        if kind != "compute":
            s, n = kind, 16
            if kind == "dma":
                s = "dm%d" % ndma[0]
                ndma[0] += 1
            elif cnt.get(s):
                wait(e, (s, cnt[s]))
        cnt[s] = cnt.get(s, 0) + n
        call().then_inc(T.sem[s], n)
        note(e, (s, cnt[s]), reads, writes)

    def run(e, reads, writes, call, cost, late=0.0, cont=False, kind="compute"):
        todo.append((e, [r for r in reads if isinstance(r, tuple)], writes, call, cont, kind, cost, late))

    def schedule():
        seen, before, tail = {}, [], {}
        for i, (e, reads, writes, *_) in enumerate(todo):
            d = set()
            for lst, w in ((reads, False), (writes, True)):
                for r in lst:
                    for a, b, row, w2, j in seen.get(r[1], []):
                        if r[1][0] == "q" or ((w or w2) and a < r[3] and r[2] < b and (row is None or r[4] is None or row == r[4])):
                            d.add(j)
            for lst, w in ((reads, False), (writes, True)):
                for r in lst:
                    h = seen.setdefault(r[1], [])
                    if r[1][0] == "q":
                        h[:] = []
                    elif w:
                        h[:] = [x for x in h if not (r[2] <= x[0] and x[1] <= r[3] and (r[4] is None or r[4] == x[2]))]
                    h.append((r[2], r[3], r[4], w, i))
            d.discard(i)
            before.append(d)
            tail.setdefault(e, []).append(i)
        free = {e: 0.0 for e in Q}

        def soonest(i, memo):
            if i not in memo:
                memo[i] = max([free[todo[i][0]]] + [done[j] if j in done else soonest(j, memo) + todo[j][6] + todo[j][7] + WAKE for j in before[i]])
            return memo[i]
        while len(done) < len(todo):
            best, memo = None, {}
            for e, mine in tail.items():
                limit = 1e9
                for i in mine[:LOOSE.get(e, 1)]:
                    t0 = soonest(i, memo)
                    if t0 + todo[i][6] <= limit + SLACK and all(j in done for j in before[i]) and (best is None or t0 < best[0]):
                        if i == mine[0] or e in "ps" or all(done[j] + MARGIN <= t0 for j in before[i] if todo[j][0] != e):
                            best = (t0, i)
                    limit = min(limit, t0)
            t0, i = best
            e, reads, writes, call, cont, kind, cost, late = todo[i]
            tail[e].remove(i)
            issue(e, reads, writes, call, cont, kind)
            free[e] = t0 + cost
            done[i] = t0 + cost + late + WAKE

    def ap(x):
        return x[0] if isinstance(x, tuple) else x

    def us(n, *sides, fix=0.0):
        if sides and all(SCRATCH[x[1]][2] in (BF, U) for x in sides):
            n = n / 2
        return fix + max(n, 64) * 1e-3

    def dma(out, in_, e="s", s="dma", after=None):
        sb = in_ if isinstance(in_, tuple) else out
        size = sb[5] * (2 if SCRATCH[sb[1]][2] == BF else 4)
        run(e, [in_, after], [out] if isinstance(out, tuple) else [], lambda: Q[e].dma_start(ap(out), ap(in_)), 0.05, 1.5 + size * 4e-4, kind=s)

    def unwrap(win, row, src, a=0):
        dma(R(win, a, a + 16 * (src[3] - src[2]), row=row), src)

    def ts(out, in0, s1, op0, s2=None, op1=None):
        if op1 is None:
            run("v", [in0, s1], [out], lambda: g.vector.tensor_scalar(out[0], in0[0], ap(s1), None, op0), us(out[5], out, in0))
        else:
            run("v", [in0, s1, s2], [out], lambda: g.vector.tensor_scalar(out[0], in0[0], ap(s1), ap(s2), op0, op1), us(out[5], out, in0))

    def tt(out, in0, in1, op):
        run("v", [in0, in1], [out], lambda: g.vector.tensor_tensor(out[0], in0[0], in1[0], op), us(out[5] * (1 if in0[1][0] == "q" else 2)))

    def cp(out, in_):
        run("v", [in_], [out], lambda: g.vector.tensor_copy(out[0], in_[0]), us(out[5], out, in_))

    def total(out, in_, op=Op.add):
        run("v", [in_], [out], lambda: g.vector.tensor_reduce(out[0], in_[0], AX.X, op), us(in_[5]))

    def fill(out, val):
        run("v", [], [out], lambda: g.vector.memset(out[0], val), us(out[5], out))

    def act(out, in_, func=AF.Identity, bias=0.0, scale=1.0, accum=None):
        w = [out] + ([accum] if accum else [])
        if accum:
            run("a", [in_, bias, scale], w, lambda: g.scalar.activation(out[0], in_[0], func, ap(bias), ap(scale), accum_out=accum[0]), us(out[5], fix=0.08))
        else:
            run("a", [in_, bias, scale], w, lambda: g.scalar.activation(out[0], in_[0], func, ap(bias), ap(scale)), us(out[5], fix=0.065))

    def gat(e, out, win, off, in1=None, op=None):
        c = us(GATHER * out[5], fix=0.06)
        if e == "a":
            run("a", [win, off], [out], lambda: g.scalar.activation(out[0], win[0].indirect(off[0]), AF.Copy), c)
        elif in1 is None:
            run("v", [win, off], [out], lambda: g.vector.tensor_copy(out[0], win[0].indirect(off[0])), c)
        else:
            run("v", [win, off, in1], [out], lambda: g.vector.tensor_tensor(out[0], win[0].indirect(off[0]), in1[0], op), c)

    def mms(terms, start=True, stop=True):
        def call():
            for i, (o, l, r) in enumerate(terms):
                ins = g.tensor.matmul(o[0], l[0], r[0], start and i == 0, stop and i == len(terms) - 1)
            return ins
        cost = sum(max(64, r[5]) * (4 if SCRATCH[r[1]][2] == F else 1) for o, l, r in terms) * 5e-4
        run("p", [x for t in terms for x in t[1:]], list({t[0][1:]: t[0] for t in terms}.values()), call, cost, cont=not start)

    def mm(out, terms, start=True, stop=True):
        mms([(out, l, r) for l, r in terms], start, stop)

    def send(t):
        rid, pid, _ = topo.addr(nxt)
        ne = len(topo.engines(core, nxt))
        land = R("XW%d" % t, 0, A)

        def call():
            g.remote_dma(land[0], T["blk%d" % t][:], T.sem["arr%d" % t], T.sem.sent, pid, rid, topo.mask(core, nxt))
            cnt["sent"] = cnt.get("sent", 0) + ne
            cnt["arr%d" % t] = ne
            hist.setdefault(land[1], []).append((0, A, None, True, ("arr%d" % t, ne), "r"))
        run("g", [R("blk%d" % t)], [land], call, 0.1, 3.5, kind="remote")

    def wrap(w, name, a, b):
        o = 144 * WN.index(w)
        return [(R("wide", o + 15 - i, o + 143 - i), R(name, a + i, b, 16)) for i in range(16)]

    def iota(out, pattern, base, cm, flt=True):
        if flt:
            run("g", [], [out], lambda: g.iota(out[0], pattern, base, cm, allow_small_or_imprecise_dtypes=True), us(2 * out[5], fix=0.13))
        else:
            run("g", [], [out], lambda: g.iota(out[0], pattern, base, cm), us(2 * out[5], fix=0.13))

    def select(out, in_, pattern, op, val, base, cm):
        run("g", [in_], [out], lambda: g.affine_select(out[0], in_[0], pattern, op, val, base, cm), us(2 * out[5], fix=0.17))

    def gcopy(out, in_):
        select(out, in_, [[0, out[5]]], Op.is_ge, 0.0, 0, 0)

    def ID(val):
        return B("idm", IDS.index(val))

    def ident(*vals):
        return [(ID(val), R("zer"), [[-1, 128]], Op.not_equal, val, 0, 1) for val in vals]

    def by_row(out, rows, pattern=((-16, 8),)):
        return [(out, out, [list(p) for p in pattern], Op.not_equal, val, -r, 1) for r, val in rows.items()]

    def weights(w, rows=None):
        o = 144 * WN.index(w)
        out = R("wide", o + 15, o + 143, 16)
        if w in ROWS:
            return by_row(out, {r: v for r, v in ROWS[w].items() if rows is None or r in rows})
        return [(out, out, [[16, 8]], Op.is_gt, EVEN[w][1], EVEN[w][0], -1), (out, out, [[16, 8]], Op.is_ge, 0.0, 15, -1)]

    def weave(*chains):
        for i in range(max(len(c) for c in chains)):
            for c in chains:
                if i < len(c):
                    (select if len(c[i]) == 7 else iota)(*c[i])

    def zero(*outs):
        return [(o, [[0, o[5]]], 0, 0) for o in outs]

    def C(k):
        return R("col", k, k + 1)

    def hi16(h, src):
        ts(h, src, C16A, Op.add, C16B, Op.subtract)

    hb, lb, cc = B("lk", 0, 256), B("lk", 1, 256), B("lk", 2, 256)

    def H(x, h, n=128):
        return R(x[1], x[2] + n * h, x[2] + n * h + n)

    def laterlists(bank):
        act(R("sq"), hb, AF.Sign, -1016.0)
        mm(R(bank, 0, 256), [(ID(128.0), lb), (ID(0.0625), hb), (ID(-64.0), cc), (ID(992.0), R("sq"))])
        mm(R(bank, 256, 512), [(ID(1.0), lb), (ID(1.0), hb), (ID(2048.0), cc)])

    def laterlists2(bank):
        ts(R("bl"), R(bank, 0, 256), 64 + 992 - 128 * OFF, Op.add)
        ts(R("sl"), R(bank, 256, 512), -OFF, Op.add)

    def near(s):
        mm(R("q%d" % s, 0, 384), [(ID(1.0), R("hc")), (ID(1.0), R("lc"))], True, False)
        mms([(B("q%d" % s, i), ID(-1.0), H(x, s)) for i in range(3) for x in (hb, lb)], False, True)

    def near2(s):
        act(B("eq", s, 384), R("q%d" % s, 0, 384), AF.Abs, -2064.0)

    def near3(s):
        act(B("ep", s, 384), B("eq", s, 384), AF.Relu, 1.0, -1.0)

    dma(R("nbi"), T.nb[:])
    dma(R("cdi"), T.cd[:])
    fill(R("PS", 0, L + 16), 0.0)
    iota(R("pi", 0, 1), [[0, 1]], 0, 1, False)
    iota(R("ew"), [[0, 16]], 0, 0)
    iota(R("zer"), [[0, 128]], 0, 0)
    act(R("PS", L + 16, 4112), R("PS", 0, L), AF.Copy)
    fill(R("wide"), 0.0)
    weave(by_row(R("ew", 0, 8), {W0: 2048.0, W0 + 1: 15 + OFF, W0 + 2: 4096.0}), ident(*IDS[:3]))
    ts(R("pi", 1, 2), R("pi", 0, 1), 15, Op.bitwise_and)
    total(R("PS", L, L + 1), R("ew", 0, 8), Op.max)
    cp(C(1), R("pi", 1, 2))
    iota(R("r16"), [[0, 2], [16, 128]], 0, 0)
    select(R("idf"), R("zer"), [[-1, 128]], Op.not_equal, 1.0, 0, 1)
    weave(weights("WTWO"), weights("FOUR"), ident(*IDS[3:7]))
    weave(by_row(R("ew", 8, 16), {HI: 2048.0, LO: 15 + OFF, CAME: 1.0, OPEN: 1.0}), weights("PTR", (HI, LO, CAME)),
          zero(R("EA", L, L + 16), *[R(w, 4096, 4112) for w in ("PA", "PB", "EA", "EB")]))

    def constants():
        weave(ident(*IDS[7:]), [(R("oneb"), [[0, 128]], 1, 0), (R("utm"), R("oneb"), [[-16, 8], [0, 16]], Op.is_ge, 0.0, 0, 1),
                                (R("blkm"), R("utm"), [[16, 8], [0, 16]], Op.is_ge, 0.0, 15, -1), (R("utm"), [[0, 128]], 0, 0),
                                (R("utm"), R("utm"), [[1, 128]], Op.is_ge, -1.0, 0, -1), (R("utm"), R("utm"), [[16, 8], [0, 16]], Op.is_ge, 0.0, 15, -1)],
              zero(R("blkf")) + by_row(R("blkf"), {JOIN: 512.0, OPEN: -512.0}, ((-16, 8), (0, 16))),
              *[weights(w) for w in WN if w not in ("WTWO", "FOUR", "PTR")])
        iota(R("rk"), [[1, 256]], 0, 0)
        iota(R("rkb"), [[1, 256]], 0, 0)
        iota(R("tab", 16, 32), [[0, 16]], 65536, 0)
        iota(R("one"), [[0, 128]], 1, 0)
        for i, val in enumerate(CST):
            select(B("cst", i), R("zer"), [[0, 128]], Op.is_gt, val, 0, 0)
        for j in range(4):
            select(B("mh", j), R("zer"), [[0, 128]], Op.is_gt, -0.5, 0, 0)
        iota(R("pw", 128, 144), [[0, 16]], 65536, 0)
        weave(zero(R("XW0", A + L, A + YO), R("XW1", A + L, A + YO), R("PT")))
    ts(R("t1"), R("nbi"), OFF, Op.add)
    hi16(hb, R("t1"))
    for s in range(2):
        unwrap("PS", W0 + 2 * s, H(hb, s))
    tt(R("l0"), R("t1"), hb, Op.subtract)
    for s in range(2):
        unwrap("PS", W0 + 2 * s + 1, B("l0", s))
    dma(R("EA", 0, L), T.x0[:], after=R("l0"))
    dma(R("thi"), T.th[:], after=R("l0"))
    ts(R("fr"), R("nbi"), 2048.0, Op.is_ge)
    mm(R("q6", 0, 256), [(ID(128.0), R("l0")), (ID(0.0625), hb), (ID(1920.0), R("fr"))])
    ts(C(2), C(1), OFF, Op.add)
    ts(C(3), C(1), -1.0, Op.mult, -2 * OFF, Op.add)
    ts(R("t2"), R("fr"), FREE + OFF, Op.mult)
    ts(R("wl"), R("q6", 0, 256), -128 * OFF, Op.add)
    act(R("nio"), R("r16"), AF.Identity, C(2))
    ts(R("cf"), R("cdi", 0, 384), 2064 + OFF, Op.add)
    tt(R("nn"), R("t2"), R("nio"), Op.max)
    act(R("hc"), R("cf"), AF.Identity, -7.5 - OFF)
    mm(R("q7", 0, 384), [(R("idf"), R("cf")), (ID(-1.0), R("hc"))])
    mm(R("q5", 0, 256), [(ID(1.0), R("l0")), (ID(15.0), R("fr"))])

    def reach(j):
        gat("va"[j // 2], B("PB", j, 1024), R("PS", 0, L + 16), B("wl", j, 64))

    def came(j):
        mm(B("q%d" % (j // 2), j % 2, 64), wrap("WTWO", "PB", 1024 * j, 1024 * j + 1024))

    def twice(j):
        mm(B("q2", j, 64), [(ID(-1.0), B("r16", j, 64))] + wrap("FOUR", "PB", 1024 * j, 1024 * j + 1024))

    def twice2(a, b):
        ts(R("el", 64 * a, 64 * b), R("q2", 64 * a, 64 * b), C(3), Op.add, 2048.0, Op.min)
    for j in (0, 2, 1, 3):
        reach(j)
    act(lb, R("q5", 0, 256))
    came(0)
    came(2)
    twice(0)
    came(3)
    came(1)
    mm(R("q6", 0, 256), [(ID(256.0), lb), (ID(0.0625), hb)], True, False)
    unwrap("PS", HI, hb)
    unwrap("PS", LO, lb)
    unwrap("PS", OPEN, R("fr"))
    total(R("PS", 4096, 4097), R("ew", 8, 16), Op.max)
    ts(C(4), C(1), 8192 + OFF, Op.add)
    ts(C(6), C(1), -1.0, Op.mult, -2064 - OFF, Op.add)
    ts(C(7), C(1), 8.0, Op.is_ge, 65536.0, Op.mult)
    ts(C(9), C(1), 128.0, Op.mult, 112.0, Op.add)
    ts(R("upto"), B("r16", 0), C(9), Op.is_le)
    cp(R("cl"), R("cdi"))
    twice2(0, 1)
    tt(H(cc, 1), R("q1", 0, 128), B("nn", 1), Op.is_equal)
    tt(H(cc, 0), R("q0", 0, 128), B("nn", 0), Op.is_equal)
    unwrap("PS", CAME, cc)
    mm(R("q6", 0, 256), [(ID(128.0), cc)], False, True)
    act(B("X", 0, 1024), B("EA", 0, 1024))
    act(R("lc"), R("q7", 0, 384))
    act(R("lz"), R("q7", 0, 384), AF.Identity, -16 - OFF)
    act(R("PA", END, END + 1), R("PS", 4096, 4097), AF.Copy)
    act(R("PB", END, END + 1), R("PS", 4096, 4097), AF.Copy)
    mm(R("q5", 0, 384), [(ID(1.0), R("hc")), (ID(1.0), R("lc"))], True, False)
    mms([(B("q5", i), ID(-1.0), B("r16", 0)) for i in range(3)], False, True)
    act(R("es"), R("q5", 0, 384), AF.Abs, C(6))
    act(R("es"), R("es"), AF.Relu, 1.0, -1.0)
    for j in (1, 2, 3):
        twice(j)
    gcopy(B("X", 1, 1024), B("EA", 1, 1024))
    constants()

    for t in range(RO):
        last = t == RO - 1
        XW = "XW%d" % t
        XF = R(XW, A, A + YO)
        FQ, RQ, LQ = ("q6", "q7", "q2", "q0"), ("q4", "q5", "q0", "q1"), ("q5", "q3")

        def first(e, j):
            gat(e, B("PA", j, 1024), R("PS"), B("wl", j, 64))
            mm(bank(0, j), wrap("PTR", "PA", 1024 * j, 1024 * j + 1024))

        def bank(k, j):
            return R(("q0", "q1", "q3", "q4")[j], 0, 64) if k == 0 else B("q%d" % (turn(k).index(j) % 2), j // 2, 64)

        def point(k, j):
            src, dst = ("PA", "PB")[(k - 1) % 2], ("PA", "PB")[k % 2]
            gat("a", B(dst, j, 1024), R(src), B("pl%d" % ((k - 1) % 2), j, 64))
            mm(bank(k, j), wrap("PTR", dst, 1024 * j, 1024 * j + 1024))

        def conv(k, j):
            ts(B("pl%d" % (k % 2), j, 64), bank(k, j), -OFF, Op.add)

        def most(k, j):
            es, ed = ("EA", "EB")[k % 2], ("EB", "EA")[k % 2]
            if k == 0 and t == 0:
                gat("v", B(ed, j, 1024), R(es, 0, L + 16), B("el", j, 64), B("X", j % 2, 1024), Op.max)
            else:
                own = B("X", j % 2, 1024) if k == 0 else B("EC", j, 1024)
                gat("v", B(ed, j, 1024), R(es), B("pl%d" % (k % 2), j, 64), own, Op.max)
            keep(k, j, ed)

        def keep(k, j, src):
            dma(B("EC", j, 1024), B(src, j, 1024), "s", "ec%d" % j)

        def fold1(j):
            mm(R("q%d" % (2 + j % 2)), [(ID(1.0), B("EA", j, 512)), (ID(-1.0), B("EA", 4 + j, 512))])
            act(B("ab", j, 512), R("q%d" % (2 + j % 2)), AF.Abs)

        def fold0(j):
            mm(R(FQ[j]), [(ID(1.0), B("X", j, 512))], True, False)

        def ended(j):
            mm(R(RQ[j]), [(R("blkf"), B("PB", j, 512)), (R("blkf"), B("PB", 4 + j, 512))], True, False)

        def fold2(j):
            mm(R(RQ[j]), [(ID(1.0), B("ab", j, 512))], False, True)
            act(B("rr", j, 512), R(RQ[j]), AF.Relu)

        def fold3(j):
            mm(R(FQ[j]), [(ID(1.0), B("ab", j, 512)), (ID(-1.0), B("rr", j, 512))], False, True)
            act(B("y32", j, 512), R(FQ[j]), AF.Identity, M1, HALF)

        def fold4(j):
            act(R(XW, A + 512 * j, A + 512 * j + 512), B("y32", j, 512), AF.Identity, -M1)
            gcopy(B("X", j, 512), R(XW, A + 512 * j, A + 512 * j + 512))

        def sums(name, a, stop=False):
            o = 144 * WN.index("SUMH")
            mms([(R("q4", 128 + i, 256, 16), R(name, a + i, a + L, 16), R("wide", o + 15, o + 143, 16)) for i in range(16)], False, stop)

        def larger(j):
            gat("v", B("EB", j, 1024), R("EA"), B("sl", j, 64), B("EC", j, 1024), Op.max)

        def largersum(j):
            mm(B(LQ[j % 2], j // 2, 64), [(R("s01"), B("idf", j % 2, 64))] + wrap("SUM", "EB", 1024 * j, 1024 * j + 1024))

        def linksum(h):
            cp(B("bh", h), R(LQ[h], 0, 128))
            unwrap("PT", HI, B("bh", h), L * h)
            tt(B("bo", h), R(LQ[h], 0, 128), B("bh", h), Op.subtract)
            unwrap("PT", LO, B("bo", h), L * h)

        def turn(k):
            return (0, 1, 2, 3) if k < K - 3 else (0, 2, 1, 3)

        def side(k, j):
            if t:
                if (k, j) == (1, 1):
                    act(R("lk", 0, 512), R("q5"))
                if (k, j) == (2, 1):
                    act(cc, R("q7", 0, 256))
            if k == K - 2 and j < 2:
                fold0(j)
            if (k, j) == (4, 1):
                laterlists("q6")
            if (k, j) == (5, 1):
                laterlists2("q6")
        if t == 0:
            ts(R("wl"), R("q6", 0, 256), -256 * OFF, Op.add)
            most(0, 0)
            first("a", 0)
            first("v", 3)
            first("a", 1)
            first("v", 2)
            conv(0, 0)
            twice2(1, 4)
            most(0, 1)
            point(1, 0)
            conv(0, 1)
            conv(0, 2)
            conv(0, 3)
            point(1, 1)
            most(0, 2)
            conv(1, 0)
            point(1, 2)
            most(0, 3)
            ts(R("thf"), R("thi"), 0.5, Op.mult)
        else:
            first("v", 3)
            first("a", 0)
            conv(0, 3)
            first("a", 1)
            most(0, 3)
            conv(0, 0)
            first("a", 2)
            most(0, 0)
            conv(0, 1)
            point(1, 0)
            point(1, 1)
            most(0, 1)
            conv(0, 2)
            conv(1, 0)
            point(1, 2)
            most(0, 2)
        conv(1, 1)
        point(1, 3)
        for k in range(1, K - 1):
            for j in range(4):
                most(k, turn(k)[j])
                conv(k + j // 2, turn(k + j // 2)[(j + 2) % 4])
                point(k + 1, turn(k + 1)[j])
                side(k, j)
        k = K - 1
        for j in range(4):
            for h in range(2):
                gat("v", B("EA", 4 * h + j, 512), R("EB"), B("pl1", 4 * h + j, 32), B("EC", 4 * h + j, 512), Op.max)
                if j == 0:
                    conv(k, 1 + 2 * h)
                if j % 2:
                    i = 2 * h + j // 2
                    keep(k, i, "EA")
            fold1(j)
            ended(j)
            fold2(j)
        mm(R("q4", 128, 256), [(R("zer"), R("zer"))], True, False)
        sums("EA", 0)
        sums("EA", L)
        sums("rr", 0, True)
        act(R("s01"), R("q4", 128, 256))
        fold0(2)
        fold0(3)
        for j in range(4):
            fold3(j)
        for j in range(4):
            fold4(j)
        larger(0)
        largersum(0)
        larger(2)
        largersum(2)
        larger(1)
        largersum(1)
        larger(3)
        linksum(0)
        largersum(3)
        linksum(1)
        if not last:
            weave(weights("PTR", (JH, JL, CH, CL, CC)))

        def back(e, j):
            gat(e, B("PA", j, 1024), R("PT", 0, 2 * L), B("bl", j, 64))
            o = 2 * (j % 2) + j // 2
            mm(B("q2", j, 64),
               [(ID(1.0), B("bh", o, 64)), (ID(1.0), B("bo", o, 64)), (ID(16384.0), B("fr", j, 64))]
               + ([(ID(-16384.0), B("jb", j, 64))] if t else []) + wrap("TWO", "PA", 1024 * j, 1024 * j + 1024))

        def mc(i, h, a=0, b=1024):
            o = 1024 * h
            gat("v", R("MC", i * L + o + a, i * L + o + b), XF, R("cl", (i * L + o + a) // 16, (i * L + o + b) // 16), R("X", o + a, o + b), Op.max)

        def mcsum(i, h):
            if h == 0:
                mm(R("q%d" % (3 + i), 0, 128),
                   [(ID(1.0), B("cst", 0)), (ID(2.0 ** 26), B("es", i)), (ID(-8192.0), R("hs")), (ID(-8192.0), R("ls"))], True, False)
            mm(B("q%d" % (3 + i), h, 64), wrap("SUMK", "MC", i * L + 1024 * h, i * L + 1024 * h + 1024), False, False)
        mm(R("q7", 0, 128), wrap("SUM", XW, A, A + L))
        act(R("hs"), R("q7", 0, 128))
        mc(0, 0)
        back("a", 0)
        back("v", 2)
        back("a", 1)
        back("a", 3)
        if t == 0:
            mm(R("q6", 0, 384), [(ID(128.0), R("lc")), (ID(0.0625), R("hc"))])
        for s in range(2):
            near(s)
            near2(s)
            near3(s)
        tt(R("ls"), R("q7", 0, 128), R("hs"), Op.subtract)
        unwrap("PT", HI, R("hs"), SC0)
        unwrap("PT", LO, R("ls"), SC0)
        mc(2, 0)
        mc(1, 0)
        if t == 0:
            ts(R("wcl"), R("q6", 0, 384), -129 - 128 * OFF, Op.add)
        ts(R("fr"), R("q2", 0, 256), R("thf", t, t + 1), Op.is_ge)
        tt(R("fb"), B("fr", 0), B("fr", 1), Op.max)
        unwrap("PT", FRE, R("fb"), SC0)
        unwrap("PT", LOW, B("fr", 0), TO0)
        if not last:
            unwrap("PS", OPEN, R("fr"))
        mm(R("q2", 0, 128), [(R("blkm"), R("fb"))])
        mm(R("q7", 0, 128), [(R("utm"), R("fb"))])
        tt(R("sw"), R("q2", 0, 128), R("upto"), Op.mult)
        run("v", [R("one"), R("q2", 0, 128)], [R("cum")],
            lambda: g.vector.tensor_tensor_scan(T.cum[:], T.one[:], T.q2[:, 0:128], 0.0, Op.mult, Op.add), us(128))
        total(C(8), R("sw"))
        act(R("cumb"), R("cum"))
        ts(B("cmp", 0, 256), R("rkb"), C(8), Op.is_ge)
        mm(R("q2", 128, 144), wrap("SUM", "cmp", 0, 256))
        tt(R("pw", 0, 128), R("q7", 0, 128), R("cum"), Op.add)
        mm(R("q6", 0, 16), [(l, R("cumb", i, 128, 8)) for i, (l, r) in enumerate(wrap("ROW0", "cmp", 0, 256)[:8])])
        act(R("tab", 0, 16), R("q6", 0, 16), AF.Identity, C(7))
        cp(R("l1", 0, 16), R("q2", 128, 144))
        cp(R("colb", 0, 16), R("q2", 128, 144))
        gat("v", B("cmp", 1, 256), R("tab"), R("l1", 0, 16), R("rk"), Op.is_le)
        mm(R("q6", 16, 32), [(ID(8.0), R("colb", 0, 16))] + wrap("SUM", "cmp", 256, 512))
        cp(R("l1", 16, 32), R("q6", 16, 32))
        cp(R("colb", 16, 32), R("q6", 16, 32))
        gat("v", B("cmp", 2, 256), R("pw"), R("l1", 16, 32), R("rk"), Op.is_le)
        mm(R("q7", 128, 144), [(ID(16.0), R("colb", 16, 32))] + wrap("SUM", "cmp", 512, 768))
        cp(R("l2"), R("q7", 128, 144))
        gat("v", R("blk%d" % t), XF, R("l2"))
        send(t)
        for s in range(2):
            mms([(R("q%d" % s, 0, 384), ID(1.0), B("ep", s, 384))] + [(B("q%d" % s, i), ID(-1.0), B("fr", s)) for i in range(3)])
            act(B("eq", s, 384), R("q%d" % s, 0, 384), AF.Relu)

        def sc(e, i, h):
            gat(e, B("SC", 2 * i + h, 1024), R("PT", SC0, SC0 + L), B("wcl", 2 * i + h, 64))
            mm(B("q%d" % (3 + i), h, 64), wrap("SWW", "SC", i * L + 1024 * h, i * L + 1024 * h + 1024), False, False)

        def key(i):
            mm(R("q%d" % (3 + i), 0, 128), [(ID(2.0 ** 26), B("eq", i)), (ID(2.0 ** 26), B("eq", 3 + i))]
               + ([(ID(i - 1.0), B("cst", 1))] if i != 1 else []) + [(ID(1.0), B("hc", i)), (ID(1.0), B("lz", i))], False, True)

        def arrival(h):
            a, b = 3 * L + 1024 * h, 3 * L + 1024 * h + 1024
            gat("v", R("MC", a, b), R(XW, 0, A), B("cl", 6 + h, 64), B("X", h, 1024), Op.max)
            mm(B("q6", h, 64), wrap("SUMK", "MC", a, b), False, False)

        def arrived(h):
            a, b = 3 * L + 1024 * h, 3 * L + 1024 * h + 1024
            gat("a", R("SC", a, b), R(XW, 0, A), B("cl", 6 + h, 64))
            mm(B("q6", h, 64), wrap("SUMN", "SC", a, b), False, h == 1)
        YQ = ("q0", "q1", "q2", "q7")

        def mixing(j):
            mm(R(YQ[j]), [(ID(0.5), R("mh")), (ID(0.5), B("X", j, 512))], True, False)

        def mixing2(j):
            mm(R(YQ[j]), [(ID(0.5), R("SC", 3 * L + 512 * j, 3 * L + 512 * j + 512))], False, True)

        def mixing3(j):
            ts(R(XW, A + YO + 512 * j, A + YO + 512 * j + 512), R(YQ[j]), M1, Op.add, M1, Op.subtract)
        for i in range(3):
            mcsum(i, 0)
        mm(R("q6", 0, 128), [(ID(1.0), B("cst", 2)), (ID(-2.0 ** 28), R("fb")), (ID(1.0), B("cst", 3)), (ID(-8192.0), R("hs")), (ID(-8192.0), R("ls"))], True, False)
        for j in range(4):
            mixing(j)
        sc("a", 0, 0)
        for a in (0, 256, 512, 768):
            mc(0, 1, a, a + 256)
        mcsum(0, 1)
        sc("a", 0, 1)
        key(0)
        for a in (0, 256, 512):
            mc(1, 1, a, a + max(a, 256))
        mcsum(1, 1)
        sc("a", 1, 0)
        sc("a", 1, 1)
        key(1)
        mc(2, 1)
        mcsum(2, 1)
        sc("a", 2, 0)
        sc("v", 2, 1)
        key(2)
        cp(R("km"), R("q3", 0, 128))
        arrival(0)
        arrived(0)
        mixing2(0)
        mixing2(1)
        tt(R("km"), R("km"), R("q4", 0, 128), Op.min)
        arrival(1)
        arrived(1)
        tt(R("ki"), R("km"), R("q5", 0, 128), Op.min)
        ts(R("ti"), R("ki"), 2047, Op.bitwise_and)
        ts(R("tq"), R("ti"), OFF, Op.add)
        hi16(R("hw"), R("tq"))
        unwrap("PT", HI, R("hw"), TO0)
        tt(R("mix"), R("q6", 0, 128), R("ki"), Op.is_lt)
        unwrap("PT", MIX, R("mix"), TO0)
        tt(R("lw"), R("tq"), R("hw"), Op.subtract)
        unwrap("PT", LO, R("lw"), TO0)

        def blend(e, h):
            gat(e, B("X", h, 1024), R(XW, A, A + YO + L), B("ml", h, 64))

        def mutual(e, h):
            gat(e, B("PA", h, 1024), R("PT", TO0, TO0 + L), B("tl", h, 64))
        mm(R("q6", 128, 256), [(ID(128.0), R("lw")), (ID(0.0625), R("hw"))])
        mm(R("q6", 256, 384), [(ID(1.0), B("r16", 0)), (ID(float(YO)), R("mix"))])
        mixing2(2)
        mixing2(3)
        mm(R("q5", 256, 384), [(ID(1.0), B("r16", 0)), (ID(-8192.0), B("fr", 0))])
        mm(R("q5", 384, 512), [(ID(1.0), B("r16", 0)), (ID(-8192.0), B("fr", 1)), (ID(8192.0), B("fr", 0))])
        act(R("wa"), R("q5", 256, 512), AF.Identity, C(4))
        if last:
            mm(R("q3", 0, 256), [(ID(1.0), hb), (ID(1.0), lb), (ID(4096.0), R("fr"))])
        else:
            mm(R("q3", 0, 256), [(ID(2048.0), R("fr")), (ID(-1.0), hb)])
            mm(R("q3", 256, 512), [(ID(31.25), R("fr")), (ID(-1.0), lb)])
            mm(R("q4", 0, 256), [(ID(1.0), R("fr")), (ID(-1.0), cc)])
            act(R("ct", 0, 512), R("q3"), AF.Relu)
            act(R("ct", 512, 768), R("q4", 0, 256), AF.Relu)
        mixing3(0)
        mixing3(1)
        ts(R("tl"), R("q6", 128, 256), -128 * OFF, Op.add)
        ts(R("ml"), R("q6", 256, 384), C(1), Op.add)
        mixing3(2)
        mixing3(3)
        if last:
            for h in range(2):
                mm(B("q4", h), [(ID(1.0), R("hw")), (ID(1.0), R("lw")), (ID(-1.0), B("cst", 1)), (ID(-16.25), R("oneb"))])
            ts(R("q3", 256, 512), R("q3", 0, 256), -OFF, Op.add, 2048.0, Op.min)
        else:
            for i, row in enumerate((CH, CL, CC)):
                dma(R("PS", 0, 4096, row=row), B("ct", i, 256), after=R("tl"))
            for h in range(2):
                mm(B("q4", 2 + h), [(ID(-1.0), R("lw")), (ID(31.25), R("oneb"))])
            mm(R("q1", 0, 128), [(ID(-1.0), R("hw")), (ID(4096.0), R("oneb"))], True, False)
        mm(R("q0", 0, 128), [(ID(-8192.0), R("mix"))], True, False)
        mutual("v", 0)
        mutual("a", 1)
        for h in range(2):
            mm(B("q0", h, 64), wrap("R0", "PA", 1024 * h, 1024 * h + 1024), False, h == 1)
        if last:
            blend("a", 0)
            dma(T.yx[:, 0:1024], B("X", 0, 1024))
            blend("a", 1)
            for h in range(2):
                tt(B("jb", h), R("q0", 0, 128), B("wa", h), Op.is_equal)
            tt(R("jj"), R("q4", 0, 256), R("jb"), Op.mult)
            tt(R("yo"), R("q3", 256, 512), R("jj"), Op.add)
            dma(T.yx[:, 1024:L], B("X", 1, 1024))
            dma(T.yn[:], R("yo"))
        else:
            jh, jl, e0 = B("jn", 0, 256), B("jn", 1, 256), B("jn", 2, 256)
            ch, cl, ca = B("ct", 0, 256), B("ct", 1, 256), B("ct", 2, 256)
            for h in range(2):
                mm(B("q1", h, 64), wrap("R1", "PA", 1024 * h, 1024 * h + 1024), False, h == 1)
            mm(R("q6", 0, 256), [(ID(256.0), lb), (ID(256.0), cl), (ID(0.0625), hb), (ID(0.0625), ch), (ID(128.0), cc), (ID(128.0), ca)], True, False)
            blend("a", 0)
            blend("a", 1)
            for h in range(2):
                tt(B("jb", h), R("q0", 0, 128), B("wa", h), Op.is_equal)
            unwrap("PS", JOIN, R("jb"))
            tt(jl, R("q4", 256, 512), R("jb"), Op.mult)
            unwrap("PS", JL, jl)
            for h in range(2):
                tt(H(jh, h), R("q1", 0, 128), B("jb", h), Op.mult)
            unwrap("PS", JH, jh)
            gcopy(B("EA", 0, 1024), B("X", 0, 1024))
            gcopy(B("EA", 2, 1024), B("X", 0, 1024))
            mm(R("q6", 0, 256), [(ID(-256.0), jl), (ID(-0.0625), jh)], False, True)
            ts(e0, jh, 2048.0, Op.is_gt)
            ts(R("wl"), R("q6", 0, 256), -256 * OFF, Op.add)
            cp(B("EA", 1, 1024), B("X", 1, 1024))
            cp(B("EA", 3, 1024), B("X", 1, 1024))
            for i in range(3):
                mm(R(("q5", "q5", "q7")[i], 256 * (i % 2), 256 * (i % 2) + 256),
                   [(ID(1.0), B("lk", i, 256)), (ID(1.0), B("ct", i, 256)), (ID(-1.0), B("jn", i, 256))] + ([] if i else [(ID(2048.0), e0)]))
    schedule()
    for s, n in cnt.items():
        if n:
            wait("g", (s, n))
